import numpy as np, ml_dtypes
CORES = [9,25,41,57]
N = 4
BF = ml_dtypes.bfloat16
W, K, T, S, ND = 4096, 256, 4, 1, 2
def stir(rng, a, n):
    r = rng.random(a.shape, dtype=np.float32)
    s = np.concatenate([np.sort(r, axis=-1), np.full(r.shape[:-1] + (1,), 2, np.float32)], axis=-1)
    return np.where(r < np.take_along_axis(s, n[..., None], -1), (a + rng.integers(1, 64, a.shape)) & 63, a)
def near(rng, pro, n, counts):
    a = pro[np.arange(8)[None, :, None], rng.integers(0, pro.shape[1], (N, 8, n))]
    return stir(rng, a, rng.choice(np.array(counts), (N, 8, n)))
def protos(rng, first):
    return stir(rng, np.repeat(first, 2, axis=1), np.full((8, 2), 3))
def parts(rng):
    pro = protos(rng, rng.integers(0, 64, (8, 1, 16)))
    return (near(rng, pro, K, [0, 1, 1, 2, 2, 3, 16]), rng.integers(0, 256, (N, 8, K, 16)), near(rng, pro, W, [0, 1, 1, 2, 3, 16]), rng.integers(0, 256, (N, 8, W, 16)),
            rng.integers(0, 256, (8, 16, 2)), rng.integers(900, 1900, (N, 8, 16)))
def tile(a):
    return np.ascontiguousarray(a.transpose(0, 1, 3, 2)).reshape(N, 128, -1).astype(np.float32).astype(BF)
def pack(x, g, lx, lm, w, lim):
    return {"xw": tile(x), "gw": tile(g), "lex": tile(lx), "mng": tile(lm),
            "wts": np.ascontiguousarray(np.broadcast_to(w.reshape(1, 128, 2), (N, 128, 2))).astype(np.int32), "th": lim.reshape(N, 128, 1).astype(np.int32)}
def setup_inputs(rng):
    return pack(*parts(rng))
def setup_inputs_spread(rng):
    pro = protos(rng, (64 * rng.random((8, 1, 16)) ** 3).astype(np.int64))
    x = near(rng, pro, K, [0, 1, 1, 2, 3, 4, 16]); lx = near(rng, pro, W, [0, 1, 1, 2, 4, 16])
    g = np.floor(256 * rng.random((N, 8, K, 1)) ** 2 * rng.random((N, 8, K, 16))).astype(np.int64)
    lm = np.floor(256 * rng.random((N, 8, W, 1)) ** 2 * rng.random((N, 8, W, 16))).astype(np.int64)
    w = np.exp2(8 * rng.random((8, 16, 2))).astype(np.int64) - 1; w = np.where(rng.random(w.shape) < 0.25, rng.integers(0, 256, w.shape), w)
    lim = np.minimum(np.exp2(4 + 8.2 * rng.random((N, 8, 16))).astype(np.int64), 4081)
    return pack(x, g, lx, lm, w, lim)
def setup_inputs_ends(rng):
    base = np.repeat(63 * rng.integers(0, 2, (8, 1, 16)), 2, axis=1); base[:, 1] = np.where(rng.random((8, 16)) < 0.15, 63 - base[:, 1], base[:, 1])
    def some(n, share):
        a = base[np.arange(8)[None, :, None], rng.integers(0, 2, (N, 8, n))]
        return np.where(rng.random(a.shape) < share, np.where(rng.random(a.shape) < 0.6, 63 - a, rng.choice(np.array([1, 31, 62]), a.shape)), a)
    def both(n):
        return 255 * np.where(rng.random((N, 8, n, 1)) < 0.5, rng.integers(0, 2, (N, 8, n, 1)), rng.integers(0, 2, (N, 8, n, 16)))
    x = some(K, 0.08); lx = some(W, 0.1); g = both(K); lm = both(W)
    w = 255 * rng.integers(0, 2, (8, 16, 2)); w[:5, 15] = 65; w[5, :, 0] = 255; w[6, 0] = 65; w[7, 14:, 0] = 65; w[7, 14:, 1] = 0
    w[4, 13, 0] = 89; w[4, 13, 1] = 0; w[4, 14, 0] = 0; w[4, 14, 1] = 227
    lim = np.full((N, 8, 16), 4081); odd = np.arange(N) % 2 == 1
    lim = np.where(odd[:, None, None] & (rng.random(lim.shape) < 0.25), 0, lim); lim[:, 0, 0] = 0
    x[:, 0, :, 0] = 63; lx[:, 0, :, 0] = 63
    x[:, 5, 1] = 63; x[:, 5, K - 1] = 63
    for i in (3, K - 2):
        x[:, 1:5, i] = 0; x[:, 1:5, i, 15] = 63
    p = (((W - 1) ** 2 >> 5) + W - 1) & (W - 1)
    lx[:, 1:5, p] = 0; lx[:, 1:5, p, 15] = 63; lx[:, 1:5, p, 13] = 63
    x[:, 4, 4] = 0; x[:, 4, 4, 13] = 46; x[:, 4, 4, 14] = 36; x[:, 4, 4, 15] = 63
    p = ((4093 * 4075 >> 5) + 4093) & (W - 1)
    lx[:, 4, p] = x[:, 4, 4]; lx[:, 4, p, 0] = 63; lx[:, 4, p + 1] = 63; lm[:, 4, p] = 255; g[:, 4, 4] = 0
    x[:, 7, 4] = 0; x[:, 7, 4, 14] = 63; g[:, 7, 4] = 0
    for i in (5, K - 1):
        x[:, 7, i] = 0; x[:, 7, i, 15] = 63; g[:, 7, i] = 255 if i == 5 else 0
    lx[:, 7, 0] = 63; lx[:, 7, W - 1] = 0; lx[:, 7, W - 1, 14:] = 63; lm[:, 7, W - 1] = 255
    g[:, 6, :, 15] = 255; lm[:, 6, :, 15] = 255; g[:, 6, :, 14] = 0; lm[:, 6, :, 14] = 0
    return pack(x, g, lx, lm, w, lim)
def setup_inputs_corners(rng):
    pro = rng.integers(0, 64, (8, 1, 16)); lx = near(rng, pro, W, [0, 0, 1]); lx[:, :, 0] = pro[:, 0]
    x = near(rng, pro, K, [0, 1, ND, ND + 1, ND + 2, 16])
    w = rng.integers(0, 256, (8, 16, 2)); w[0] = 0; w[1] = 255; w[2, :, 0] = 0; w[2, :, 1] = 255; w[3, :, 1] = w[3, :, 0]; w[4, :15] = 0; w[4, 15] = 255; w[5, 1:] = 0; w[5, 0] = 255
    w[6] = 255 * rng.integers(0, 2, (16, 2)); w = w[rng.permutation(8)]
    def mean(n):
        return np.where(rng.random((N, 8, n, 1)) < 0.6, 255 * rng.integers(0, 2, (N, 8, n, 1)), rng.integers(0, 256, (N, 8, n, 16)))
    case = (np.arange(8)[None, :] + np.arange(N)[:, None] + rng.integers(0, 5)) % 5; case = case[:, :, None]
    lim = np.where(case == 0, 0, np.where(case == 1, 4081, np.where(case == 2, 4081 * rng.integers(0, 2, (N, 8, 16)), np.where(case == 3, 1, rng.integers(900, 1900, (N, 8, 16))))))
    return pack(x, mean(K), lx, mean(W), w, lim)
def setup_inputs_ties(rng):
    pro = rng.integers(0, 64, (8, 1, 16)); far = np.where(rng.permutation(8) < 4, 0, rng.integers(130, 251, 8)).reshape(8, 1, 1)
    b = rng.integers(0, 255 - far, (8, 1, 16)); side = rng.integers(0, 2, (8, 1, 16))
    x = near(rng, pro, K, [0, 1, 1, 1]); lx = near(rng, pro, W, [0, ND, ND, ND + 1])
    g = b + far * side + rng.integers(0, 2, (N, 8, K, 16)); lm = b + far * (1 - side) + rng.integers(0, 2, (N, 8, W, 16))
    lim = np.where(far[:, 0] == 0, rng.integers(5, 13, (N, 8, 16)), 16 * far[:, 0] + rng.integers(-3, 5, (N, 8, 16)))
    return pack(x, g, lx, lm, rng.integers(0, 256, (8, 16, 2)), lim)
def setup_inputs_alike(rng):
    o = rng.permutation(64); al = o[:4]; kinds = (rng.integers(0, 4, (8, 1, 16)) + (rng.random((8, 6, 16)) < 0.12) * rng.integers(1, 4, (8, 6, 16))) & 3
    pro = al[kinds]; x = near(rng, pro, K, [0]); lx = near(rng, pro, W, [0])
    g = rng.integers(0, 256, (N, 8, K, 16)); lm = rng.integers(0, 256, (N, 8, W, 16)); w = rng.integers(0, 256, (8, 16, 2))
    even = (np.arange(N) % 2 == 0)[:, None, None]
    lim = np.where((rng.random((N, 8, 1)) < 0.6) | even, 4081, rng.integers(900, 1900, (N, 8, 16)))
    two = np.sort(o[4:12].reshape(4, 2), axis=1); spot = np.arange(W); four = [int(e) for e in rng.permutation(8)[:4]]
    for e in four:
        lx[:, e] = pro[e, 0]; lx[:, e, :, 0] = two[spot & 3, 1]; lx[:, e, :, 14] = spot & 63; lx[:, e, :, 15] = spot >> 6
        w[e] = 0; w[e, 14, 0] = 1; w[e, 15, 0] = 64; lim[:, e] = 4081
    for r in range(N):
        j = rng.permutation(W >> 1)[:K]
        put = [4 * (j >> 1) + 2 + (j & 1),
               np.full(K, 4 * rng.integers(0, W >> 2) + 2 + rng.integers(0, 2)),
               4 * rng.permutation(W >> 2)[:K] + (np.arange(K) >= 256),
               np.repeat(4 * rng.permutation(W >> 2)[:K >> 1] + (np.arange(K >> 1) & 3), 2)]
        for e, p in zip(four, put):
            x[r, e] = pro[e, 0]; x[r, e, :, 0] = two[p & 3, 0]; x[r, e, :, 14] = p & 63; x[r, e, :, 15] = p >> 6
    e = four[2]
    g[:, e] = rng.integers(0, 41, (N, K, 16)) + 200 * even; lm[:, e] = rng.integers(0, 41, (N, W, 16)); lim[:, e] = rng.integers(700, 2500, (N, 16))
    return pack(x, g, lx, lm, w, lim)
def check_inputs(d):
    bad = []
    for k, lo, hi in (("xw", 0, 63), ("gw", 0, 255), ("lex", 0, 63), ("mng", 0, 255), ("wts", 0, 255), ("th", 0, 4081)):
        a = np.asarray(d[k]).astype(np.float64)
        if not (np.min(a) >= lo and np.max(a) <= hi): bad.append("range of " + k)
        elif np.any(a != np.floor(a)): bad.append("whole numbers of " + k)
    a = np.asarray(d["wts"])
    if np.any(a != a[:1]): bad.append("wts alike on all ranks")
    return bad
def visit(t, x, g, lx, lm, w, lim):
    p = w[..., :1] * x; u = (np.add.reduce(p, axis=1, keepdims=True) - p) & (W - 1)
    p = w[..., 1:] * x; u2 = (np.add.reduce(p, axis=1, keepdims=True) - p) & (W - 1)
    h = (((u * u2) >> 5) + u) & (W - 1)
    c = np.take_along_axis(lx, h.reshape(8, 1, 16 * K), 2).reshape(8, 16, 16, K)
    m = np.take_along_axis(lm, h.reshape(8, 1, 16 * K), 2).reshape(8, 16, 16, K)
    differ = np.add.reduce((c != x[:, :, None, :]).astype(np.int32), axis=1)
    far = np.add.reduce(np.abs(m - g[:, :, None, :]), axis=1)
    lane = np.arange(16); b = c[:, lane, lane, :]
    pair = (b != x) & (differ <= ND + 1)
    has = np.any(pair, axis=1); f = np.argmax(pair, axis=1)[:, None, :]
    def at(a):
        return np.take_along_axis(a, f, 1)[:, 0]
    xa, xb, hf = at(x), at(b), at(h)
    free = at((far < lim).astype(np.int32)) == 1
    pc = 64 * np.minimum(xa, xb) + np.maximum(xa, xb)
    flag = np.zeros(4096, bool); flag[pc[has & ~free]] = True
    merge = has & free & ~flag[pc]
    mf = np.take_along_axis(lm, hf[:, None, :], 2)
    row = lane[None, :, None]
    xn = np.where((row == f) & merge[:, None, :], np.minimum(x, b), x)
    xn = np.where((row == t) & ~has[:, None, :], b, xn)
    gn = np.where(merge[:, None, :], (g + mf) >> 1, g)
    for e in range(8):
        for i in np.flatnonzero(merge[e])[::-1]:
            lx[e, :, hf[e, i]] = xn[e, :, i]; lm[e, :, hf[e, i]] = gn[e, :, i]
    x[...] = xn; g[...] = gn
def reference(xw, gw, lex, mng, wts, th):
    x = xw.astype(np.float32).astype(np.int32).reshape(N, 8, 16, K); g = gw.astype(np.float32).astype(np.int32).reshape(N, 8, 16, K)
    lx = lex.astype(np.float32).astype(np.int32).reshape(N, 8, 16, W); lm = mng.astype(np.float32).astype(np.int32).reshape(N, 8, 16, W)
    w = wts.astype(np.int32).reshape(N, 8, 16, 2); lim = th.astype(np.int32).reshape(N, 8, 16, 1)
    for t in range(T):
        for r in range(N):
            v = (r + S * t) % N; visit(t, x[r], g[r], lx[v], lm[v], w[v], lim[v])
    return {"yx": x.reshape(N, 128, K).astype(np.float32).astype(BF), "yg": g.reshape(N, 128, K).astype(np.float32).astype(BF),
            "yl": lx.reshape(N, 128, W).astype(np.float32).astype(BF), "ym": np.add.reduce(lm, axis=3).reshape(N, 128, 1).astype(np.float32)}

@@ -1,0 +1,496 @@
+from concourse.mybir import AluOpType as A, ActivationFunctionType as F, AxisListType as X
+
+K = 256
+W = 4096
+NV = 4
+CH = 64
+PARTS = ((0, 128), (128, 256))
+CFG = {"h0": 64, "xs": 6, "cs": 4, "eqs": 6}
+
+SCRATCH = {}
+
+
+def _buf(name, cols, dtype, where="sbuf", rows=128):
+    SCRATCH[name] = (where, [rows, cols], dtype)
+
+
+for _t in range(NV + 1):
+    _buf("xin%d" % _t, K, "bfloat16")
+    _buf("gin%d" % _t, K, "bfloat16")
+for _d, _l in (
+        ("bfloat16", (("xo", NV * K), ("go", NV * K), ("zt", NV * 128), ("lx", W + K), ("lm", W + K), ("ones", 128), ("ones64", 512),
+                      ("bo1", 128), ("bo", 128), ("idn", 128), ("lt", 128), ("gt", 128), ("c1", 128), ("c2", 128), ("c3", 128),
+                      ("zb", 128), ("za", 128), ("e1", 128), ("bd", 128), ("w1", 128), ("w2", 128), ("lk", 2048), ("lb", 2048),
+                      ("blt", 2048), ("nid", 128), ("nid64", 128), ("idh", 128), ("nidh", 128), ("n4096", 128), ("cb", 128),
+                      ("oz", 512), ("ra", 512), ("io0", 64), ("ion", 64), ("fb", 512), ("cg", 4096), ("d", 4096), ("pair", K),
+                      ("ep", K), ("gs", K), ("ca", 2 * K), ("dg", K), ("gm", K), ("en", K), ("ndx", K), ("xa", 1024), ("xh", 1024),
+                      ("chh", 1024), ("h1", 64), ("tb", K), ("rm", K), ("f", K), ("eq", 4096), ("ea", 2048), ("ls", K))),
+        ("float16", (("lb16", 2048), ("id16", 128), ("nid16", 128), ("bo16", 128), ("bo16a", 128), ("h16", K), ("eh", K), ("t1", 3 * K))),
+        ("int32", (("wti", 2), ("thi", 1), ("jci", 1), ("jcj", 1), ("pr", K), ("p2", K), ("hs", K), ("h", K), ("xi", 16), ("x3", 16))),
+        ("uint16", (("hu", K), ("hq", 16), ("of", 16), ("hr", K), ("so", 16))),
+        ("float32", (("thr", NV), ("wf", 2), ("thc", 1), ("jc", 1), ("io16", 16), ("md", 16), ("ltc", 16), ("dm0", 16), ("dmp", 16),
+                     ("nb", 1), ("u2s", K), ("hqf", 16), ("qs", 48), ("xq", 16), ("q1", 16), ("thq", 16), ("cq", 16), ("off", 16),
+                     ("nf", 16), ("dg1", K), ("dg2", K), ("mt", K), ("yv", K), ("nm", 16), ("hm0", 16), ("hqm", 16), ("hqs", 16),
+                     ("lq2", 16), ("so0", 16), ("sm", 3)))):
+    for _n, _c in _l:
+        _buf(_n, _c, _d)
+for _n in ("pu1", "pu2", "pxp", "ppa", "ppb", "pq", "pval", "ph"):
+    _buf(_n, 512, "float32", "psum")
+
+SEMAPHORES = ["v", "s", "p", "gc", "loc"]
+SEMAPHORES += ["ld%d" % _i for _i in range(6)] + ["st%d" % _i for _i in range(4)]
+SEMAPHORES += ["ax%d" % _i for _i in range(1, NV + 1)] + ["ag%d" % _i for _i in range(1, NV + 1)]
+
+
+def tracker(g, T):
+    queue = {"V": g.vector, "S": g.scalar, "P": g.tensor, "G": g, "Y": g.sync}
+    own = {"V": "v", "S": "s", "P": "p", "G": "gc"}
+    total = {}
+    know = {q: {} for q in queue}
+    log = {}
+
+    def span(a):
+        if len(a) == 1:
+            return a[0], 0, SCRATCH[a[0]][1][1]
+        return a
+
+    def need(q, reads, writes):
+        found = []
+        for wr, accs in ((False, reads), (True, writes)):
+            for a in accs:
+                name, lo, hi = span(a)
+                bank = SCRATCH[name][0] == "psum"
+                for r in log.get(name, ()):
+                    lap = r["lo"] < hi and lo < r["hi"]
+                    if bank and r["q"] != q:
+                        found.append(r)
+                    elif lap and (r["wr"] or wr):
+                        if bank and q == "P":
+                            continue
+                        found.append(r)
+        return found
+
+    def wait(q, found):
+        for r in sorted(found, key=lambda r: -r["seq"]):
+            if know[q].get(r["sem"], 0) < r["val"]:
+                queue[q].wait_ge(T.sem[r["sem"]], r["val"])
+                for s, v in r["clock"].items():
+                    know[q][s] = max(know[q].get(s, 0), v)
+
+    seq = [0]
+
+    def note(q, sem, val, clock, reads, writes, dma):
+        seq[0] += 1
+        for wr, accs in ((True, writes), (False, reads)):
+            for a in accs:
+                name, lo, hi = span(a)
+                rows = log.setdefault(name, [])
+                if wr:
+                    rows[:] = [r for r in rows if not (lo <= r["lo"] and r["hi"] <= hi)]
+                rows.append({"q": q, "sem": sem, "val": val, "clock": clock, "lo": lo, "hi": hi, "wr": wr, "dma": dma, "seq": seq[0]})
+
+    def op(q, call, reads=(), writes=()):
+        wait(q, need(q, reads, writes))
+        sem = own[q]
+        call(queue[q]).then_inc(T.sem[sem], 1)
+        total[sem] = total.get(sem, 0) + 1
+        clock = dict(know[q])
+        clock[sem] = total[sem]
+        note(q, sem, total[sem], clock, reads, writes, False)
+
+    def dma(q, call, sem, reads=(), writes=()):
+        wait(q, need(q, reads, writes))
+        call(queue[q]).then_inc(T.sem[sem], 16)
+        clock = dict(know[q])
+        clock[sem] = 16
+        note("dma", sem, 16, clock, reads, writes, True)
+
+    def arrive(sem, val, writes):
+        note("dma", sem, val, {sem: val}, (), writes, True)
+
+    def ready(q, reads):
+        wait(q, need(q, reads, ()))
+
+    def finish():
+        for sem, q in (("v", "G"), ("s", "G"), ("p", "G"), ("gc", "V")):
+            if know[q].get(sem, 0) < total[sem]:
+                queue[q].wait_ge(T.sem[sem], total[sem])
+
+    return op, dma, arrive, ready, finish
+
+
+def rank_program(g, core, T, topo):
+    rank = T.rank_of(core)
+    if rank is None:
+        return
+    op, dma, arrive, ready, finish = tracker(g, T)
+
+    def v(a):
+        return T[a[0]][:] if len(a) == 1 else T[a[0]][:, a[1]:a[2]] if len(a) == 3 else T[a[0]][:, a[1]:a[2]:a[3]]
+
+    def rw(*a):
+        return tuple(x[:3] for x in a if isinstance(x, tuple))
+
+    def sc(x):
+        return v(x) if isinstance(x, tuple) else x
+
+    def ts(out, i0, s1, o0, s2=None, o1=None):
+        if o1 is None:
+            op("V", lambda e: e.tensor_scalar(v(out), v(i0), sc(s1), None, o0), rw(i0, s1), rw(out))
+        else:
+            op("V", lambda e: e.tensor_scalar(v(out), v(i0), sc(s1), sc(s2), o0, o1), rw(i0, s1, s2), rw(out))
+
+    def tt(out, a, b, o):
+        op("V", lambda e: e.tensor_tensor(v(out), v(a), v(b), o), rw(a, b), rw(out))
+
+    def gat(out, win, offs, b, o):
+        op("V", lambda e: e.tensor_tensor(v(out), v(win).indirect(v(offs)), v(b), o), rw(win, offs, b), rw(out))
+
+    def cp(out, a):
+        op("V", lambda e: e.tensor_copy(v(out), v(a)), rw(a), rw(out))
+
+    def scat(win, offs, a):
+        op("V", lambda e: e.tensor_copy(v(win).indirect(v(offs)), v(a)), rw(offs, a), rw(win))
+
+    def fill(out, c):
+        op("V", lambda e: e.memset(v(out), c), (), rw(out))
+
+    def act(out, a, fn, bias=None, scale=None, offs=None, acc=None):
+        kw = {}
+        if bias is not None:
+            kw["bias"] = sc(bias)
+        if scale is not None:
+            kw["scale"] = scale
+        if acc is not None:
+            kw["accum_out"] = v(acc)
+        src = v(a) if offs is None else v(a).indirect(v(offs))
+        op("S", lambda e: e.activation(v(out), src, fn, **kw), rw(a, bias, offs), rw(out, acc))
+
+    def mm(out, l, rh, st=True, sp=True):
+        op("P", lambda e: e.matmul(v(out), v(l), v(rh), start=st, stop=sp), rw(l, rh), rw(out))
+
+    def to_q(out, lname, src, st=True, sp=True):
+        for b in range(16):
+            op("P", lambda e: e.matmul(v(out), T[lname][:, 128 * b:128 * b + 128], T[src[0]][:, src[1] + b:src[2]:16],
+                                       start=st and b == 0, stop=sp and b == 15), ((lname,), src), rw(out))
+
+    def load(q, out, src, sem):
+        dma(q, lambda e: e.dma_start(v(out), src[:]), sem, (), (out,))
+
+    load("S", ("xin0",), T.xw, "ld0")
+    load("Y", ("wti",), T.wts, "ld1")
+    load("Y", ("lx", 0, W), T.lex, "ld2")
+    load("S", ("thi",), T.th, "ld3")
+    load("Y", ("gin0",), T.gw, "ld4")
+    load("Y", ("lm", 0, W), T.mng, "ld5")
+
+    fill(("ones",), 1.0)
+    fill(("ones64",), 1.0)
+
+    def sel(out, i, pat, o, base, cm, rows=128):
+        op("G", lambda e: e.affine_select(T[out][0:rows, :], T[i][0:rows, :], pat, o, 0.0, base, cm), ((i,),), ((out,),))
+
+    def iota(out, pat, base, cm, **kw):
+        op("G", lambda e: e.iota(T[out][:], pat, base, cm, **kw), (), ((out,),))
+
+    small = {"allow_small_or_imprecise_dtypes": True}
+    sel("bo1", "ones", [[-16, 8], [0, 16]], A.is_ge, 0, 1)
+    sel("bo", "bo1", [[16, 8], [0, 16]], A.is_ge, 15, -1)
+    sel("idn", "ones", [[-1, 128]], A.is_equal, 0, 1)
+    iota("jci", [[0, 1]], 0, 1)
+    iota("io16", [[1, 16]], 0, 0, **small)
+    sel("lt", "bo", [[1, 128]], A.is_gt, 0, -1)
+    sel("gt", "bo", [[-1, 128]], A.is_gt, 0, 1)
+    iota("io0", [[1, 64]], 0, 0, **small)
+    iota("ion", [[1, 64]], -64, 0, **small)
+    iota("dm0", [[16, 16]], W, 0, **small)
+    sel("ra", "ones64", [[-1, 4], [0, 8], [-4, 16]], A.is_equal, 0, 1, 64)
+
+    fill(("cb",), 4160.0)
+    fill(("oz", 0, K), 1.0)
+    fill(("oz", K, 2 * K), 0.0)
+    fill(("lk",), 0.0)
+    ts(("n4096",), ("idn",), -4096.0, A.mult)
+    tt(("bd",), ("bo",), ("idn",), A.subtract)
+    ts(("c1",), ("idn",), -17.0, A.mult)
+    cp(("wf",), ("wti",))
+    ts(("w1",), ("bd",), ("wf", 0, 1), A.mult)
+    ts(("w2",), ("bd",), ("wf", 1, 2), A.mult)
+    tt(("e1",), ("bo",), ("c1",), A.add)
+    fill(("lb",), 0.0)
+
+    def blocks(out, src):
+        for k in range(16):
+            act((out, 128 * k + k, 128 * (k + 1), 16), (src, k, 128, 16), F.Copy)
+
+    def consts2():
+        ts(("c2",), ("lt",), 2.0, A.mult)
+        ts(("c3",), ("lt",), 64.0, A.mult)
+        tt(("zb",), ("c2",), ("idn",), A.subtract)
+        tt(("c2",), ("c3",), ("c1",), A.add)
+        tt(("za",), ("c2",), ("gt",), A.add)
+        for t in range(NV):
+            act(("zt", 128 * t, 128 * t + 128), ("zb",), F.Copy)
+        for t in range(NV):
+            act(("zt", 128 * t + t, 128 * t + 128, 16), ("za", t, 128, 16), F.Copy)
+        ts(("jcj",), ("jci",), 15, A.bitwise_and)
+        cp(("id16",), ("idn",))
+        cp(("jc",), ("jcj",))
+        ts(("thc",), ("thi",), -2048.0, A.add, 1 / 64.0, A.mult)
+        ts(("md",), ("io16",), ("jc",), A.is_equal)
+        ts(("thr",), ("md", 0, NV), -0.5, A.add)
+
+    def consts3():
+        cp(("lb16",), ("lb",))
+        ts(("nid",), ("idn",), -1.0, A.mult)
+        cp(("bo16",), ("bo",))
+        ts(("bo16a",), ("bo",), 32.0, A.mult)
+        ts(("nb",), ("jc",), -4.0, A.mult, -1.5, A.add)
+        ts(("nid16",), ("idn",), -1.0, A.mult)
+        ts(("nid64",), ("idn",), -1 / 64.0, A.mult)
+        ts(("idh",), ("idn",), 0.5, A.mult)
+        ts(("nidh",), ("idn",), -0.5, A.mult)
+        ts(("dmp",), ("dm0",), ("jc",), A.add)
+        ts(("ltc",), ("io16",), ("jc",), A.is_gt)
+        for b in range(16):
+            ts(("blt", 128 * b, 128 * b + 128), ("bo",), ("ltc", b, b + 1), A.mult)
+
+    nxt = T.cores[(rank + 1) % len(T.cores)]
+    rid, pid = topo.addr(nxt)[0], topo.addr(nxt)[1]
+    mask = topo.mask(core, nxt)
+    neng = len(topo.engines(core, nxt))
+
+    def send(src, dst, sem):
+        ready("G", (src,))
+        g.remote_dma(T[dst][:], v(src), T.sem[sem], T.sem.loc, pid, rid, mask)
+
+    lex, mng = ("lx", 0, W), ("lm", 0, W)
+    late = [consts3]
+
+    for t in range(NV):
+        XI, GI = ("xin%d" % t,), ("gin%d" % t,)
+        XO, GO = ("xo", K * t, K * t + K), ("go", K * t, K * t + K)
+        if t:
+            arrive("ax%d" % t, neng, (XI,))
+            arrive("ag%d" % t, neng, (GI,))
+        u1, u2, r1, r2 = ("pu1", 0, K), ("pu2", 0, K), ("pval", 0, K), ("ppa", 0, K)
+        for u in (u2, u1, r2, r1):
+            mm(u, ("cb",), ("oz", 0, K), True, False)
+        mm(u2, ("w2",), XI, False, True)
+        mm(u1, ("w1",), XI, False, True)
+        mm(r2, ("w2",), XI, False, False)
+        mm(r1, ("w1",), XI, False, False)
+        act(("fb", K, 2 * K), u2, F.Identity, -2047.5 / 4096, 1 / 4096.0)
+        ts(("fb", 0, K), u1, 1 / 4096.0, A.mult, -2047.5 / 4096, A.add)
+        mm(r2, ("n4096",), ("fb", K, 2 * K), False, True)
+        mm(r1, ("n4096",), ("fb", 0, K), False, True)
+        mm(("pxp", 0, K), ("idn",), XI)
+        spans = ((0, CFG["h0"]), (CFG["h0"], K))
+        for c0, c1 in spans:
+            act(("u2s", c0, c1), ("ppa", c0, c1), F.Copy)
+        for c0, c1 in spans:
+            tt(("pr", c0, c1), ("u2s", c0, c1), ("pval", c0, c1), A.mult)
+            ts(("p2", c0, c1), ("pr", c0, c1), 5, A.arith_shift_right, 4095, A.bitwise_and)
+            tt(("hs", c0, c1), ("p2", c0, c1), ("pval", c0, c1), A.add)
+            ts(("h", c0, c1), ("hs", c0, c1), 4095, A.bitwise_and)
+            cp(("hu", c0, c1), ("h", c0, c1))
+        if t == 0:
+            blocks("lk", "e1")
+            blocks("lb", "bo")
+            consts2()
+        for c in range(0, K, CH):
+            act(("cg", 16 * c, 16 * (c + CH)), lex, F.Copy, offs=("hu", c, c + CH))
+
+        def compare(c):
+            bank = "ppa" if c < PARTS[0][1] else "ppb"
+            o = c - (0 if bank == "ppa" else PARTS[1][0])
+            for k in range(16):
+                d0 = 16 * c + k * CH
+                tt(("d", d0, d0 + CH), ("cg", 16 * c + k, 16 * (c + CH), 16), ("pxp", c, c + CH), A.not_equal)
+            for k in range(16):
+                d0 = 16 * c + k * CH
+                mm((bank, o, o + CH), ("lk", 128 * k, 128 * k + 128), ("d", d0, d0 + CH), k == 0, k == 15)
+
+        def pairs(p):
+            p0, p1 = PARTS[p]
+            bank, n = ("ppa", "ppb")[p], p1 - p0
+            ts(("pair", p0, p1), (bank, 0, n), -13.5, A.is_lt)
+            mm((bank, n, 2 * n), ("zt", 128 * t, 128 * t + 128), ("pair", p0, p1))
+
+        def lanes(p):
+            p0, p1 = PARTS[p]
+            bank, n = ("ppa", "ppb")[p], p1 - p0
+            ts(("ep", p0, p1), (bank, n, 2 * n), ("thr", t, t + 1), A.is_lt)
+            tt(("eh", p0, p1), ("ep", p0, p1), ("pu1", p0, p1), A.mult)
+            to_q(("pq", p0 // 16, p1 // 16), "lb16", ("eh", p0, p1))
+
+        def lanes2(p):
+            p0, p1 = PARTS[p]
+            bank, n = ("ppa", "ppb")[p], p1 - p0
+            ts(("t1", K + p0, K + p1), (bank, n, 2 * n), -0.5, A.is_lt, -64.0, A.mult)
+            tt(("t1", p0, p1), ("ep", p0, p1), ("pxp", p0, p1), A.mult)
+            ts(("t1", 2 * K + p0, 2 * K + p1), ("t1", K + p0, K + p1), ("thc",), A.mult)
+
+        def places(p):
+            a0, a1 = PARTS[p][0] // 16, PARTS[p][1] // 16
+            ts(("hq", a0, a1), ("pq", a0, a1), 2048.0, A.add)
+
+        def dist(p):
+            p0, p1 = PARTS[p]
+            bank, n = ("ppa", "ppb")[p], p1 - p0
+            act(("gs", p0, p1), mng, F.Copy, offs=("hq", p0 // 16, p1 // 16))
+            mm((bank, 0, n), ("nid",), ("gin%d" % t, p0, p1), True, False)
+            mm((bank, 0, n), ("idn",), ("gs", p0, p1), False, True)
+            act(("ca", K + p0, K + p1), (bank, 0, n), F.Abs)
+            act(("dg1", p0, p1), (bank, 0, n), F.Identity, -0.25, 0.5)
+
+        def letter(p):
+            p0, p1 = PARTS[p]
+            gat(("ca", p0, p1), lex, ("hq", p0 // 16, p1 // 16), ("ep", p0, p1), A.mult)
+
+        ts(("h16",), ("hu",), -2048.0, A.add)
+        compare(0)
+        mm(("pu1", 0, K), ("id16",), ("h16",))
+        for job in late:
+            job()
+        late = []
+        compare(CH)
+        if PARTS[0][1] == 2 * CH:
+            pairs(0)
+        compare(2 * CH)
+        if PARTS[0][1] == 3 * CH:
+            pairs(0)
+        lanes(0)
+        lanes2(0)
+        compare(3 * CH)
+        places(0)
+        pairs(1)
+        dist(0)
+        letter(0)
+        lanes(1)
+        lanes2(1)
+        to_q(("ph", 0, 48), "lb16", ("t1", 0, 3 * K))
+        places(1)
+        dist(1)
+        letter(1)
+        cp(("qs",), ("ph", 0, 48))
+        tt(("xq",), ("qs", 0, 16), ("qs", 16, 32), A.add)
+        for a in range(CFG["xs"]):
+            act(("xa", 64 * a, 64 * a + 64), ("ion",), F.Abs, ("xq", a, a + 1), -1.0)
+        if CFG["xs"]:
+            act(("xh", 0, 64 * CFG["xs"]), ("xa", 0, 64 * CFG["xs"]), F.Relu, 1.0, -1.0)
+        ts(("q1",), ("qs", 16, 32), -32.0, A.mult)
+        ts(("xi",), ("xq",), 64.0, A.mult)
+        tt(("thq",), ("q1",), ("qs", 32, 48), A.subtract)
+        ts(("x3",), ("xi",), 192, A.bitwise_and)
+        for a in range(CFG["xs"], 16):
+            ts(("xh", 64 * a, 64 * a + 64), ("ion",), ("xq", a, a + 1), A.is_equal)
+        to_q(("pq", 32, 48), "lb", ("ca", 0, K))
+        to_q(("pq", 48, 64), "lb", ("ca", K, 2 * K))
+        cp(("cq",), ("pq", 32, 48))
+        tt(("nf",), ("pq", 48, 64), ("thq",), A.is_ge)
+        ns = 16 - CFG["cs"]
+        for a in range(ns, 16):
+            act(("xa", 64 * a, 64 * a + 64), ("io0",), F.Abs, ("cq", a, a + 1), -1.0)
+        for a in range(ns, 16):
+            act(("chh", 64 * a, 64 * a + 64), ("xa", 64 * a, 64 * a + 64), F.Relu, ("nf", a, a + 1), -1.0)
+        for a in range(ns):
+            ts(("chh", 64 * a, 64 * a + 64), ("io0",), ("cq", a, a + 1), A.is_equal, ("nf", a, a + 1), A.mult)
+        mm(("pxp", K, 2 * K), ("id16",), ("t1", 0, K), True, False)
+        mm(("pxp", K, 2 * K), ("nid",), ("ca", 0, K), False, True)
+        mm(("pval", K, 2 * K), ("bo16",), ("t1", 0, K))
+        act(("mt",), ("pval", K, 2 * K), F.Abs, ("nb",))
+        act(("rm",), ("mt",), F.Relu, 32768.0, -16384.0)
+        act(("dg2",), ("dg1",), F.Identity, 12582912.0)
+        for a in range(16):
+            x, c = ("xh", 64 * a, 64 * a + 64), ("chh", 64 * a, 64 * a + 64)
+            for l, r in ((x, c), (c, x)):
+                op("P", lambda e: e.matmul(T.ph[0:64, 0:64], v(l), v(r), start=a == 0 and l is x, stop=a == 15 and l is c),
+                   (l, r), (("ph", 0, 64),))
+        tt(("off",), ("cq",), ("x3",), A.add)
+        cp(("of",), ("off",))
+        tt(("en",), ("pxp", K, 2 * K), ("t1", K, 2 * K), A.mult)
+        act(("ndx",), ("en",), F.Relu, None, -1 / 64.0)
+        op("V", lambda e: e.tensor_scalar(T.h1[0:64, :], T.ph[0:64, 0:64], 1.0, None, A.min), (("ph", 0, 64),), (("h1",),))
+        for q in range(4):
+            op("P", lambda e: e.matmul(T.ph[:, K + 64 * q:K + 64 * q + 64], T.ra[0:64, 128 * q:128 * q + 128], T.h1[0:64, :],
+                                       start=True, stop=True), (("ra",), ("h1",)), (("ph", K + 64 * q, K + 64 * q + 64),))
+        act(("tb",), ("ph", K, 2 * K), F.Copy)
+        val = ("pval", 0, K)
+        mm(val, ("bo",), ("ca", K, 2 * K), True, False)
+        mm(val, ("bo16",), ("t1", 2 * K, 3 * K), False, False)
+        mm(val, ("bo16a",), ("t1", K, 2 * K), False, False)
+        mm(("pu1", 0, K), ("idn",), XI, True, False)
+        mm(("pu1", 0, K), ("idn",), ("ca", 0, K), False, False)
+        mm(("pu1", 0, K), ("nid16",), ("t1", 0, K), False, False)
+        mm(("pu1", 0, K), ("nid64",), ("en",), False, True)
+        to_q(("pq", 80, 96), "lb", ("ca", K, 2 * K), True, False)
+        gat(("f",), ("tb",), ("of",), ("rm",), A.mult)
+        mm(val, ("bo",), ("f",), False, True)
+        act(("pu1", K, 2 * K), val, F.Relu, None, -64.0)
+        tt(("yv",), ("ndx",), ("pu1", K, 2 * K), A.min)
+        tt(XO, ("pu1", 0, K), ("yv",), A.subtract)
+        send(XO, "xin%d" % (t + 1), "ax%d" % (t + 1))
+        act(("pu2", K, 2 * K), val, F.Sign, 0.5)
+        to_q(("pq", 80, 96), "lb", ("f", 0, K), False)
+        mm(("ppb", 0, K), ("bo16",), ("eh",))
+        cp(("hqf",), ("hq",))
+        ts(("hr",), ("ppb", 0, K), 2048.0, A.add)
+        tt(("nm",), ("pq", 80, 96), ("thq",), A.is_ge)
+        tt(("hm0",), ("nm",), ("dmp",), A.mult)
+        tt(("hqm",), ("hm0",), ("hqf",), A.max)
+        nv = 16 - CFG["eqs"]
+        if nv < 16:
+            ts(("hqs", nv, 16), ("hqm", nv, 16), -2048.0, A.add)
+        for a in range(nv, 16):
+            e0 = 128 * (a - 8)
+            act(("ea", e0, e0 + K - 16 * a), ("ppb", 16 * a, K), F.Abs, ("hqs", a, a + 1), -1.0)
+        for a in range(nv, 16):
+            e0 = 128 * (a - 8)
+            act(("eq", 272 * a, 256 * a + 256), ("ea", e0, e0 + K - 16 * a), F.Relu, 1.0, -1.0)
+        for a in range(nv):
+            ts(("eq", 272 * a, 256 * a + 256), ("hr", 16 * a, K), ("hqm", a, a + 1), A.is_equal)
+        mm(("ph", 0, K), ("bo",), ("oz", K, 2 * K), True, False)
+        for a in range(15):
+            mm(("ph", 16 * a + 16, K), ("bo",), ("eq", 272 * a + 16, 256 * a + 256), False, False)
+        for b in range(16):
+            op("P", lambda e: e.matmul(T.ph[:, b:K:16], T.blt[:, 128 * b:128 * b + 128], T.eq[:, b:4096:272], start=False, stop=False),
+               (("blt",), ("eq",)), (("ph", 0, K),))
+        mm(("ph", 0, K), ("bo",), ("oz", K, 2 * K), False, True)
+        act(("dg",), ("dg2",), F.Identity, -12582912.0)
+        tt(("gm",), ("dg",), ("pu2", K, 2 * K), A.mult)
+        act(("ls",), ("ph", 0, K), F.Copy, None, 512.0)
+        to_q(("pq", 64, 80), "lb", ("ls", 0, K))
+        mm(("pxp", K, 2 * K), ("idn",), GI, True, False)
+        mm(("pxp", K, 2 * K), ("idh",), ("dg",), False, False)
+        mm(("pxp", K, 2 * K), ("nidh",), ("gm",), False, True)
+        act(GO, ("pxp", K, 2 * K), F.Copy)
+        send(GO, "gin%d" % (t + 1), "ag%d" % (t + 1))
+        tt(("lq2",), ("pq", 64, 80), ("dmp",), A.min)
+        tt(("so0",), ("hqm",), ("lq2",), A.max)
+        cp(("so",), ("so0",))
+        scat(("lx",), ("so",), XO)
+
+        def meanings(GO=GO):
+            scat(("lm",), ("so",), GO)
+        late.append(meanings)
+
+    def store(q, y, a, sem):
+        dma(q, lambda e: e.dma_start(y[:], v(a)), sem, (a,), ())
+
+    for job in late:
+        job()
+    arrive("ax%d" % NV, neng, (("xin%d" % NV,),))
+    arrive("ag%d" % NV, neng, (("gin%d" % NV,),))
+    store("Y", T.yx, ("xin%d" % NV,), "st1")
+    store("Y", T.yl, lex, "st0")
+    store("Y", T.yg, ("gin%d" % NV,), "st2")
+    h = W // 2
+    op("V", lambda e: e.tensor_reduce(T.sm[:, 0:1], T.lm[:, 0:h], X.X, A.add), (("lm", 0, h),), (("sm", 0, 1),))
+    act(("cg", 0, h), ("lm", h, W), F.Copy, acc=("sm", 1, 2))
+    tt(("sm", 2, 3), ("sm", 0, 1), ("sm", 1, 2), A.add)
+    store("S", T.ym, ("sm", 2, 3), "st3")
+    for i in range(4):
+        g.wait_ge(T.sem["st%d" % i], 16)
+    g.wait_ge(T.sem.loc, 2 * NV * neng)
+    finish()

@@ -5,7 +5,7 @@ W = 4096
 NV = 4
 CH = 64
 PARTS = ((0, 128), (128, 256))
-CFG = {"h0": 64, "xs": 6, "cs": 4, "eqs": 6}
+CFG = {"h0": 64, "xs": 6, "cs": 4, "eqs": 6, "chains": (((0, 64), (64, 128)), ((128, 192), (192, 256))), "lm": 1}
 
 SCRATCH = {}
 
@@ -28,9 +28,9 @@ for _d, _l in (
         ("float16", (("lb16", 2048), ("id16", 128), ("nid16", 128), ("bo16", 128), ("bo16a", 128), ("h16", K), ("eh", K), ("t1", 3 * K))),
         ("int32", (("wti", 2), ("thi", 1), ("jci", 1), ("jcj", 1), ("pr", K), ("p2", K), ("hs", K), ("h", K), ("xi", 16), ("x3", 16))),
         ("uint16", (("hu", K), ("hq", 16), ("of", 16), ("hr", K), ("so", 16))),
-        ("float32", (("thr", NV), ("wf", 2), ("thc", 1), ("jc", 1), ("io16", 16), ("md", 16), ("ltc", 16), ("dm0", 16), ("dmp", 16),
-                     ("nb", 1), ("u2s", K), ("hqf", 16), ("qs", 48), ("xq", 16), ("q1", 16), ("thq", 16), ("cq", 16), ("off", 16),
-                     ("nf", 16), ("dg1", K), ("dg2", K), ("mt", K), ("yv", K), ("nm", 16), ("hm0", 16), ("hqm", 16), ("hqs", 16),
+        ("float32", (("thr", NV), ("wf", 2), ("thc", 1), ("jc", 1), ("io16", 16), ("md", 16), ("dm0", 16), ("dmp", 16),
+                     ("nb", 1), ("u2s", K), ("hqf", 16), ("qs", 48), ("xq", 16), ("q1", 16), ("thq", 16), ("th2", 16), ("q2", 16), ("hqx", 16), ("sq", 16), ("cq", 16), ("off", 16),
+                     ("nf", 16), ("dg1", K), ("dg2", K), ("mt", K), ("yv", K), ("nm", 16), ("hqm", 16), ("hqs", 16),
                      ("lq2", 16), ("so0", 16), ("sm", 3)))):
     for _n, _c in _l:
         _buf(_n, _c, _d)
@@ -251,9 +251,9 @@ def rank_program(g, core, T, topo):
         ts(("idh",), ("idn",), 0.5, A.mult)
         ts(("nidh",), ("idn",), -0.5, A.mult)
         ts(("dmp",), ("dm0",), ("jc",), A.add)
-        ts(("ltc",), ("io16",), ("jc",), A.is_gt)
         for b in range(16):
-            ts(("blt", 128 * b, 128 * b + 128), ("bo",), ("ltc", b, b + 1), A.mult)
+            op("G", lambda e: e.affine_select(T.blt[:, 128 * b:128 * b + 128], T.bo[:], [[16, 8], [0, 16]], A.is_gt, 0.0, b, -1),
+               (("bo",),), (("blt", 128 * b, 128 * b + 128),))
 
     nxt = T.cores[(rank + 1) % len(T.cores)]
     rid, pid = topo.addr(nxt)[0], topo.addr(nxt)[1]
@@ -265,6 +265,7 @@ def rank_program(g, core, T, topo):
         g.remote_dma(T[dst][:], v(src), T.sem[sem], T.sem.loc, pid, rid, mask)
 
     lex, mng = ("lx", 0, W), ("lm", 0, W)
+    soon = []
     late = [consts3]
 
     for t in range(NV):
@@ -288,12 +289,20 @@ def rank_program(g, core, T, topo):
         spans = ((0, CFG["h0"]), (CFG["h0"], K))
         for c0, c1 in spans:
             act(("u2s", c0, c1), ("ppa", c0, c1), F.Copy)
-        for c0, c1 in spans:
-            tt(("pr", c0, c1), ("u2s", c0, c1), ("pval", c0, c1), A.mult)
-            ts(("p2", c0, c1), ("pr", c0, c1), 5, A.arith_shift_right, 4095, A.bitwise_and)
-            tt(("hs", c0, c1), ("p2", c0, c1), ("pval", c0, c1), A.add)
-            ts(("h", c0, c1), ("hs", c0, c1), 4095, A.bitwise_and)
-            cp(("hu", c0, c1), ("h", c0, c1))
+        for job in soon:
+            job()
+        soon = []
+        for chain in CFG["chains"]:
+            for c0, c1 in chain:
+                tt(("pr", c0, c1), ("u2s", c0, c1), ("pval", c0, c1), A.mult)
+            for c0, c1 in chain:
+                ts(("p2", c0, c1), ("pr", c0, c1), 5, A.arith_shift_right, 4095, A.bitwise_and)
+            for c0, c1 in chain:
+                tt(("hs", c0, c1), ("p2", c0, c1), ("pval", c0, c1), A.add)
+            for c0, c1 in chain:
+                ts(("h", c0, c1), ("hs", c0, c1), 4095, A.bitwise_and)
+            for c0, c1 in chain:
+                cp(("hu", c0, c1), ("h", c0, c1))
         if t == 0:
             blocks("lk", "e1")
             blocks("lb", "bo")
@@ -349,6 +358,10 @@ def rank_program(g, core, T, topo):
             gat(("ca", p0, p1), lex, ("hq", p0 // 16, p1 // 16), ("ep", p0, p1), A.mult)
 
         ts(("h16",), ("hu",), -2048.0, A.add)
+        if CFG["lm"] or not t:
+            for job in late:
+                job()
+            late = []
         compare(0)
         mm(("pu1", 0, K), ("id16",), ("h16",))
         for job in late:
@@ -361,8 +374,8 @@ def rank_program(g, core, T, topo):
         if PARTS[0][1] == 3 * CH:
             pairs(0)
         lanes(0)
-        lanes2(0)
         compare(3 * CH)
+        lanes2(0)
         places(0)
         pairs(1)
         dist(0)
@@ -375,25 +388,23 @@ def rank_program(g, core, T, topo):
         letter(1)
         cp(("qs",), ("ph", 0, 48))
         tt(("xq",), ("qs", 0, 16), ("qs", 16, 32), A.add)
-        for a in range(CFG["xs"]):
+        nx, ns = 16 - CFG["xs"], 16 - CFG["cs"]
+        for a in range(nx, 16):
             act(("xa", 64 * a, 64 * a + 64), ("ion",), F.Abs, ("xq", a, a + 1), -1.0)
-        if CFG["xs"]:
-            act(("xh", 0, 64 * CFG["xs"]), ("xa", 0, 64 * CFG["xs"]), F.Relu, 1.0, -1.0)
+        act(("xh", 64 * nx, 1024), ("xa", 64 * nx, 1024), F.Relu, 1.0, -1.0)
         ts(("q1",), ("qs", 16, 32), -32.0, A.mult)
         ts(("xi",), ("xq",), 64.0, A.mult)
         tt(("thq",), ("q1",), ("qs", 32, 48), A.subtract)
         ts(("x3",), ("xi",), 192, A.bitwise_and)
-        for a in range(CFG["xs"], 16):
+        for a in range(nx):
             ts(("xh", 64 * a, 64 * a + 64), ("ion",), ("xq", a, a + 1), A.is_equal)
-        to_q(("pq", 32, 48), "lb", ("ca", 0, K))
-        to_q(("pq", 48, 64), "lb", ("ca", K, 2 * K))
+        to_q(("pq", 32, 64), "lb", ("ca", 0, 2 * K))
         cp(("cq",), ("pq", 32, 48))
         tt(("nf",), ("pq", 48, 64), ("thq",), A.is_ge)
-        ns = 16 - CFG["cs"]
         for a in range(ns, 16):
-            act(("xa", 64 * a, 64 * a + 64), ("io0",), F.Abs, ("cq", a, a + 1), -1.0)
+            act(("xa", 64 * (a - ns), 64 * (a - ns) + 64), ("io0",), F.Abs, ("cq", a, a + 1), -1.0)
         for a in range(ns, 16):
-            act(("chh", 64 * a, 64 * a + 64), ("xa", 64 * a, 64 * a + 64), F.Relu, ("nf", a, a + 1), -1.0)
+            act(("chh", 64 * a, 64 * a + 64), ("xa", 64 * (a - ns), 64 * (a - ns) + 64), F.Relu, ("nf", a, a + 1), -1.0)
         for a in range(ns):
             ts(("chh", 64 * a, 64 * a + 64), ("io0",), ("cq", a, a + 1), A.is_equal, ("nf", a, a + 1), A.mult)
         mm(("pxp", K, 2 * K), ("id16",), ("t1", 0, K), True, False)
@@ -408,14 +419,19 @@ def rank_program(g, core, T, topo):
                 op("P", lambda e: e.matmul(T.ph[0:64, 0:64], v(l), v(r), start=a == 0 and l is x, stop=a == 15 and l is c),
                    (l, r), (("ph", 0, 64),))
         tt(("off",), ("cq",), ("x3",), A.add)
+        tt(("th2",), ("thq",), ("pq", 48, 64), A.subtract)
         cp(("of",), ("off",))
         tt(("en",), ("pxp", K, 2 * K), ("t1", K, 2 * K), A.mult)
         act(("ndx",), ("en",), F.Relu, None, -1 / 64.0)
+        ts(("q2",), ("th2",), 0.0, A.is_le, 8192.0, A.mult)
+        cp(("hqf",), ("hq",))
+        mm(("ppb", 0, K), ("bo16",), ("eh",))
         op("V", lambda e: e.tensor_scalar(T.h1[0:64, :], T.ph[0:64, 0:64], 1.0, None, A.min), (("ph", 0, 64),), (("h1",),))
         for q in range(4):
             op("P", lambda e: e.matmul(T.ph[:, K + 64 * q:K + 64 * q + 64], T.ra[0:64, 128 * q:128 * q + 128], T.h1[0:64, :],
                                        start=True, stop=True), (("ra",), ("h1",)), (("ph", K + 64 * q, K + 64 * q + 64),))
         act(("tb",), ("ph", K, 2 * K), F.Copy)
+        tt(("hqx",), ("q2",), ("hqf",), A.add)
         val = ("pval", 0, K)
         mm(val, ("bo",), ("ca", K, 2 * K), True, False)
         mm(val, ("bo16",), ("t1", 2 * K, 3 * K), False, False)
@@ -424,24 +440,18 @@ def rank_program(g, core, T, topo):
         mm(("pu1", 0, K), ("idn",), ("ca", 0, K), False, False)
         mm(("pu1", 0, K), ("nid16",), ("t1", 0, K), False, False)
         mm(("pu1", 0, K), ("nid64",), ("en",), False, True)
-        to_q(("pq", 80, 96), "lb", ("ca", K, 2 * K), True, False)
         gat(("f",), ("tb",), ("of",), ("rm",), A.mult)
         mm(val, ("bo",), ("f",), False, True)
-        act(("pu1", K, 2 * K), val, F.Relu, None, -64.0)
-        tt(("yv",), ("ndx",), ("pu1", K, 2 * K), A.min)
+        ts(("hr",), ("ppb", 0, K), 2048.0, A.add)
+        act(("pu2", K, 2 * K), val, F.Relu, None, -64.0)
+        tt(("yv",), ("ndx",), ("pu2", K, 2 * K), A.min)
         tt(XO, ("pu1", 0, K), ("yv",), A.subtract)
         send(XO, "xin%d" % (t + 1), "ax%d" % (t + 1))
-        act(("pu2", K, 2 * K), val, F.Sign, 0.5)
-        to_q(("pq", 80, 96), "lb", ("f", 0, K), False)
-        mm(("ppb", 0, K), ("bo16",), ("eh",))
-        cp(("hqf",), ("hq",))
-        ts(("hr",), ("ppb", 0, K), 2048.0, A.add)
-        tt(("nm",), ("pq", 80, 96), ("thq",), A.is_ge)
-        tt(("hm0",), ("nm",), ("dmp",), A.mult)
-        tt(("hqm",), ("hm0",), ("hqf",), A.max)
+        act(("pval", K, 2 * K), val, F.Sign, 0.5)
+        to_q(("pq", 80, 96), "lb", ("f", 0, K))
         nv = 16 - CFG["eqs"]
-        if nv < 16:
-            ts(("hqs", nv, 16), ("hqm", nv, 16), -2048.0, A.add)
+        tt(("sq",), ("hqx",), ("pq", 80, 96), A.add)
+        ts(("hqs", nv, 16), ("sq", nv, 16), -2048.0, A.add)
         for a in range(nv, 16):
             e0 = 128 * (a - 8)
             act(("ea", e0, e0 + K - 16 * a), ("ppb", 16 * a, K), F.Abs, ("hqs", a, a + 1), -1.0)
@@ -449,7 +459,10 @@ def rank_program(g, core, T, topo):
             e0 = 128 * (a - 8)
             act(("eq", 272 * a, 256 * a + 256), ("ea", e0, e0 + K - 16 * a), F.Relu, 1.0, -1.0)
         for a in range(nv):
-            ts(("eq", 272 * a, 256 * a + 256), ("hr", 16 * a, K), ("hqm", a, a + 1), A.is_equal)
+            ts(("eq", 272 * a, 256 * a + 256), ("hr", 16 * a, K), ("sq", a, a + 1), A.is_equal)
+        tt(("nm",), ("pq", 80, 96), ("th2",), A.is_ge)
+        tt(("nm",), ("nm",), ("dmp",), A.mult)
+        tt(("hqm",), ("nm",), ("hqf",), A.max)
         mm(("ph", 0, K), ("bo",), ("oz", K, 2 * K), True, False)
         for a in range(15):
             mm(("ph", 16 * a + 16, K), ("bo",), ("eq", 272 * a + 16, 256 * a + 256), False, False)
@@ -458,14 +471,17 @@ def rank_program(g, core, T, topo):
                (("blt",), ("eq",)), (("ph", 0, K),))
         mm(("ph", 0, K), ("bo",), ("oz", K, 2 * K), False, True)
         act(("dg",), ("dg2",), F.Identity, -12582912.0)
-        tt(("gm",), ("dg",), ("pu2", K, 2 * K), A.mult)
+        tt(("gm",), ("dg",), ("pval", K, 2 * K), A.mult)
         act(("ls",), ("ph", 0, K), F.Copy, None, 512.0)
         to_q(("pq", 64, 80), "lb", ("ls", 0, K))
-        mm(("pxp", K, 2 * K), ("idn",), GI, True, False)
-        mm(("pxp", K, 2 * K), ("idh",), ("dg",), False, False)
-        mm(("pxp", K, 2 * K), ("nidh",), ("gm",), False, True)
-        act(GO, ("pxp", K, 2 * K), F.Copy)
-        send(GO, "gin%d" % (t + 1), "ag%d" % (t + 1))
+
+        def new_meanings(GI=GI, GO=GO, t=t):
+            mm(("pu2", 0, K), ("idn",), GI, True, False)
+            mm(("pu2", 0, K), ("idh",), ("dg",), False, False)
+            mm(("pu2", 0, K), ("nidh",), ("gm",), False, True)
+            act(GO, ("pu2", 0, K), F.Copy)
+            send(GO, "gin%d" % (t + 1), "ag%d" % (t + 1))
+        soon.append(new_meanings)
         tt(("lq2",), ("pq", 64, 80), ("dmp",), A.min)
         tt(("so0",), ("hqm",), ("lq2",), A.max)
         cp(("so",), ("so0",))
@@ -478,7 +494,7 @@ def rank_program(g, core, T, topo):
     def store(q, y, a, sem):
         dma(q, lambda e: e.dma_start(y[:], v(a)), sem, (a,), ())
 
-    for job in late:
+    for job in soon + late:
         job()
     arrive("ax%d" % NV, neng, (("xin%d" % NV,),))
     arrive("ag%d" % NV, neng, (("gin%d" % NV,),))

@@ -5,7 +5,7 @@ W = 4096
 NV = 4
 CH = 64
 PARTS = ((0, 128), (128, 256))
-CFG = {"h0": 64, "xs": 6, "cs": 4, "eqs": 6, "chains": (((0, 64), (64, 128)), ((128, 192), (192, 256))), "lm": 1}
+CFG = {"xs": 6, "cs": 4, "eqs": 6, "chains": (((0, 64),), ((64, 128), (128, 192), (192, 256))), "lm": 1, "gv": 1, "xk": 3, "vs": 16, "go": 1}
 
 SCRATCH = {}
 
@@ -20,20 +20,22 @@ for _t in range(NV + 1):
 for _d, _l in (
         ("bfloat16", (("xo", NV * K), ("go", NV * K), ("zt", NV * 128), ("lx", W + K), ("lm", W + K), ("ones", 128), ("ones64", 512),
                       ("bo1", 128), ("bo", 128), ("idn", 128), ("lt", 128), ("gt", 128), ("c1", 128), ("c2", 128), ("c3", 128),
-                      ("zb", 128), ("za", 128), ("e1", 128), ("bd", 128), ("w1", 128), ("w2", 128), ("lk", 2048), ("lb", 2048),
-                      ("blt", 2048), ("nid", 128), ("nid64", 128), ("idh", 128), ("nidh", 128), ("n4096", 128), ("cb", 128),
+                      ("zb", 128), ("za", 128), ("e1", 128), ("bd", 128), ("w1", 256), ("w2", 128), ("lk", 2048), ("lb", 2048),
+                      ("bow", 128), ("thl", K), ("nid", 128), ("idx", 384), ("bo64", 128), ("n4096", 256), ("cb", 256), ("xb", K), ("nx", K),
                       ("oz", 512), ("ra", 512), ("io0", 64), ("ion", 64), ("fb", 512), ("cg", 4096), ("d", 4096), ("pair", K),
                       ("ep", K), ("gs", K), ("ca", 2 * K), ("dg", K), ("gm", K), ("en", K), ("ndx", K), ("xa", 1024), ("xh", 1024),
-                      ("chh", 1024), ("h1", 64), ("tb", K), ("rm", K), ("f", K), ("eq", 4096), ("ea", 2048), ("ls", K))),
-        ("float16", (("lb16", 2048), ("id16", 128), ("nid16", 128), ("bo16", 128), ("bo16a", 128), ("h16", K), ("eh", K), ("t1", 3 * K))),
-        ("int32", (("wti", 2), ("thi", 1), ("jci", 1), ("jcj", 1), ("pr", K), ("p2", K), ("hs", K), ("h", K), ("xi", 16), ("x3", 16))),
+                      ("chh", 1024), ("h1", 64), ("tb", K), ("rm", K), ("f", K), ("ea", 2048), ("ls", K))),
+        ("float16", (("lb16", 2048), ("id16", 128), ("nid16", 128), ("bo16", 384), ("h16", K), ("eh", K))),
+        ("int32", (("wti", 2), ("thi", 1), ("jci", 1), ("jcj", 1), ("pr", K), ("p2", K), ("h", K), ("xi", 16), ("x3", 16))),
         ("uint16", (("hu", K), ("hq", 16), ("of", 16), ("hr", K), ("so", 16))),
-        ("float32", (("thr", NV), ("wf", 2), ("thc", 1), ("jc", 1), ("io16", 16), ("md", 16), ("dm0", 16), ("dmp", 16),
-                     ("nb", 1), ("u2s", K), ("hqf", 16), ("qs", 48), ("xq", 16), ("q1", 16), ("thq", 16), ("th2", 16), ("q2", 16), ("hqx", 16), ("sq", 16), ("cq", 16), ("off", 16),
+        ("float32", (("thr", NV), ("wf", 2), ("thc", 1), ("jc", 1), ("io16", 16), ("md", 16), ("dm0", 16), ("dmp", 16), ("dmq", 16), ("pw", 16),
+                     ("nb", 1), ("u2s", K), ("hqf", 16), ("qs", 48), ("xq", 16), ("q1", 16), ("thq", 16), ("th2", 16), ("q2", 16), ("hqx", 16), ("sq", 16), ("cq", 16),
                      ("nf", 16), ("dg1", K), ("dg2", K), ("mt", K), ("yv", K), ("nm", 16), ("hqm", 16), ("hqs", 16),
-                     ("lq2", 16), ("so0", 16), ("sm", 3)))):
+                     ("lq2", 16), ("sm", 3)))):
     for _n, _c in _l:
         _buf(_n, _c, _d)
+SCRATCH["t1"] = ("sbuf", [128, 3, K], "float16")
+SCRATCH["eq"] = ("sbuf", [128, 16, 272], "bfloat16")
 for _n in ("pu1", "pu2", "pxp", "ppa", "ppb", "pq", "pval", "ph"):
     _buf(_n, 512, "float32", "psum")
 
@@ -126,6 +128,8 @@ def rank_program(g, core, T, topo):
     op, dma, arrive, ready, finish = tracker(g, T)
 
     def v(a):
+        if a[0] == "t1":
+            return T.t1[:, a[1] // K, a[1] % K:a[1] % K + a[2] - a[1]]
         return T[a[0]][:] if len(a) == 1 else T[a[0]][:, a[1]:a[2]] if len(a) == 3 else T[a[0]][:, a[1]:a[2]:a[3]]
 
     def rw(*a):
@@ -206,16 +210,19 @@ def rank_program(g, core, T, topo):
     iota("dm0", [[16, 16]], W, 0, **small)
     sel("ra", "ones64", [[-1, 4], [0, 8], [-4, 16]], A.is_equal, 0, 1, 64)
 
-    fill(("cb",), 4160.0)
+    fill(("cb", 0, 128), 4160.0)
+    fill(("cb", 128, 256), 67584.0)
     fill(("oz", 0, K), 1.0)
     fill(("oz", K, 2 * K), 0.0)
     fill(("lk",), 0.0)
-    ts(("n4096",), ("idn",), -4096.0, A.mult)
+    ts(("n4096", 0, 128), ("idn",), -4096.0, A.mult)
+    ts(("n4096", 128, 256), ("idn",), -131072.0, A.mult)
     tt(("bd",), ("bo",), ("idn",), A.subtract)
     ts(("c1",), ("idn",), -17.0, A.mult)
     cp(("wf",), ("wti",))
-    ts(("w1",), ("bd",), ("wf", 0, 1), A.mult)
+    ts(("w1", 0, 128), ("bd",), ("wf", 0, 1), A.mult)
     ts(("w2",), ("bd",), ("wf", 1, 2), A.mult)
+    ts(("w1", 128, 256), ("bd",), ("wf", 0, 1), A.mult, 32.0, A.mult)
     tt(("e1",), ("bo",), ("c1",), A.add)
     fill(("lb",), 0.0)
 
@@ -243,17 +250,25 @@ def rank_program(g, core, T, topo):
     def consts3():
         cp(("lb16",), ("lb",))
         ts(("nid",), ("idn",), -1.0, A.mult)
-        cp(("bo16",), ("bo",))
-        ts(("bo16a",), ("bo",), 32.0, A.mult)
+        cp(("bo16", 0, 128), ("bo",))
+        ts(("bo16", 128, 256), ("bo",), 64.0, A.mult)
+        ts(("bo16", 256, 384), ("bo",), 2048.0, A.mult)
+        ts(("bo64",), ("bo",), 64.0, A.mult)
         ts(("nb",), ("jc",), -4.0, A.mult, -1.5, A.add)
         ts(("nid16",), ("idn",), -1.0, A.mult)
-        ts(("nid64",), ("idn",), -1 / 64.0, A.mult)
-        ts(("idh",), ("idn",), 0.5, A.mult)
-        ts(("nidh",), ("idn",), -0.5, A.mult)
+        for i, c in enumerate((-1 / 64.0, 0.5, -0.5)):
+            ts(("idx", 128 * i, 128 * i + 128), ("idn",), c, A.mult)
         ts(("dmp",), ("dm0",), ("jc",), A.add)
-        for b in range(16):
-            op("G", lambda e: e.affine_select(T.blt[:, 128 * b:128 * b + 128], T.bo[:], [[16, 8], [0, 16]], A.is_gt, 0.0, b, -1),
-               (("bo",),), (("blt", 128 * b, 128 * b + 128),))
+        ts(("dmq",), ("dmp",), 1 / 16.0, A.mult)
+
+    def consts4():
+        fill(("rm",), 0.5)
+        fill(("rm", 0, K, 16), 32768.0)
+        op("V", lambda e: e.tensor_tensor_scan(v(("thl",)), v(("rm",)), v(("oz", K, 2 * K)), 2.0 ** -13, A.mult, A.add),
+           (("rm",), ("oz", K, 2 * K)), (("thl",),))
+        tt(("pw",), ("md",), ("thl", 0, 16), A.mult)
+        op("V", lambda e: e.tensor_reduce(v(("sm", 0, 1)), v(("pw",)), X.X, A.add), (("pw",),), (("sm", 0, 1),))
+        ts(("bow",), ("bo",), ("sm", 0, 1), A.mult, 0.5, A.mult)
 
     nxt = T.cores[(rank + 1) % len(T.cores)]
     rid, pid = topo.addr(nxt)[0], topo.addr(nxt)[1]
@@ -266,7 +281,7 @@ def rank_program(g, core, T, topo):
 
     lex, mng = ("lx", 0, W), ("lm", 0, W)
     soon = []
-    late = [consts3]
+    late = [consts3, consts4]
 
     for t in range(NV):
         XI, GI = ("xin%d" % t,), ("gin%d" % t,)
@@ -274,41 +289,46 @@ def rank_program(g, core, T, topo):
         if t:
             arrive("ax%d" % t, neng, (XI,))
             arrive("ag%d" % t, neng, (GI,))
-        u1, u2, r1, r2 = ("pu1", 0, K), ("pu2", 0, K), ("pval", 0, K), ("ppa", 0, K)
-        for u in (u2, u1, r2, r1):
-            mm(u, ("cb",), ("oz", 0, K), True, False)
-        mm(u2, ("w2",), XI, False, True)
-        mm(u1, ("w1",), XI, False, True)
-        mm(r2, ("w2",), XI, False, False)
-        mm(r1, ("w1",), XI, False, False)
-        act(("fb", K, 2 * K), u2, F.Identity, -2047.5 / 4096, 1 / 4096.0)
-        ts(("fb", 0, K), u1, 1 / 4096.0, A.mult, -2047.5 / 4096, A.add)
-        mm(r2, ("n4096",), ("fb", K, 2 * K), False, True)
-        mm(r1, ("n4096",), ("fb", 0, K), False, True)
+        wide = ((0, CH, "pu1", "ppa", "pval"), (CH, K, "pu2", "ph", "ppb"))
+        for c0, c1, bu, b2, b1 in wide:
+            n = c1 - c0
+            for i, w in ((1, ("w2",)), (0, ("w1", 0, 128))):
+                mm((bu, n * (1 - i), n * (2 - i)), w, ("xin%d" % t, c0, c1))
+            for i in (1, 0):
+                act(("fb", K * i + c0, K * i + c1), (bu, n * (1 - i), n * (2 - i)), F.Identity, 130 - 2047.5 / 4096, 1 / 4096.0)
+        for c0, c1, bu, b2, b1 in wide:
+            n = c1 - c0
+            for r, i, q, w in (((b2, 0, n), 1, 0, ("w2",)), ((b1, 0, n), 0, 0, ("w1", 0, 128)), ((b1, n, 2 * n), 0, 128, ("w1", 128, 256))):
+                mm(r, ("cb", q, q + 128), ("oz", 0, n), True, False)
+                mm(r, w, ("xin%d" % t, c0, c1), False, False)
+                mm(r, ("n4096", q, q + 128), ("fb", K * i + c0, K * i + c1), False, True)
+            act(("u2s", c0, c1), (b2, 0, n), F.Copy)
         mm(("pxp", 0, K), ("idn",), XI)
-        spans = ((0, CFG["h0"]), (CFG["h0"], K))
-        for c0, c1 in spans:
-            act(("u2s", c0, c1), ("ppa", c0, c1), F.Copy)
-        for job in soon:
-            job()
-        soon = []
+
+        def um(c0, c1, q):
+            b, o, n = ("pval", 0, CH) if c1 <= CH else ("ppb", CH, K - CH)
+            return (b, c0 - o + n * q, c1 - o + n * q)
+
         for chain in CFG["chains"]:
             for c0, c1 in chain:
-                tt(("pr", c0, c1), ("u2s", c0, c1), ("pval", c0, c1), A.mult)
+                tt(("pr", c0, c1), ("u2s", c0, c1), um(c0, c1, 0), A.mult)
             for c0, c1 in chain:
-                ts(("p2", c0, c1), ("pr", c0, c1), 5, A.arith_shift_right, 4095, A.bitwise_and)
+                tt(("p2", c0, c1), ("pr", c0, c1), um(c0, c1, 1), A.add)
             for c0, c1 in chain:
-                tt(("hs", c0, c1), ("p2", c0, c1), ("pval", c0, c1), A.add)
-            for c0, c1 in chain:
-                ts(("h", c0, c1), ("hs", c0, c1), 4095, A.bitwise_and)
+                ts(("h", c0, c1), ("p2", c0, c1), 5, A.arith_shift_right, 4095, A.bitwise_and)
             for c0, c1 in chain:
                 cp(("hu", c0, c1), ("h", c0, c1))
+            for job in soon:
+                job()
+            soon = []
         if t == 0:
             blocks("lk", "e1")
             blocks("lb", "bo")
             consts2()
+        vs = K - CFG["vs"]
         for c in range(0, K, CH):
-            act(("cg", 16 * c, 16 * (c + CH)), lex, F.Copy, offs=("hu", c, c + CH))
+            e1 = min(c + CH, vs)
+            act(("cg", 16 * c, 16 * e1), lex, F.Copy, offs=("hu", c, e1))
 
         def compare(c):
             bank = "ppa" if c < PARTS[0][1] else "ppb"
@@ -338,6 +358,9 @@ def rank_program(g, core, T, topo):
             bank, n = ("ppa", "ppb")[p], p1 - p0
             ts(("t1", K + p0, K + p1), (bank, n, 2 * n), -0.5, A.is_lt, -64.0, A.mult)
             tt(("t1", p0, p1), ("ep", p0, p1), ("pxp", p0, p1), A.mult)
+
+        def lanes3(p):
+            p0, p1 = PARTS[p]
             ts(("t1", 2 * K + p0, 2 * K + p1), ("t1", K + p0, K + p1), ("thc",), A.mult)
 
         def places(p):
@@ -351,7 +374,32 @@ def rank_program(g, core, T, topo):
             mm((bank, 0, n), ("nid",), ("gin%d" % t, p0, p1), True, False)
             mm((bank, 0, n), ("idn",), ("gs", p0, p1), False, True)
             act(("ca", K + p0, K + p1), (bank, 0, n), F.Abs)
-            act(("dg1", p0, p1), (bank, 0, n), F.Identity, -0.25, 0.5)
+
+        def dist_v(p):
+            p0, p1 = PARTS[p]
+            gat(("gs", p0, p1), mng, ("hq", p0 // 16, p1 // 16), ("gin%d" % t, p0, p1), A.subtract)
+            act(("ca", K + p0, K + p1), ("gs", p0, p1), F.Abs)
+
+        def first_q(p):
+            for b in range(16):
+                op("P", lambda e: e.matmul(T.ph[:, 24 * p:24 * p + 24], T.lb16[:, 128 * b:128 * b + 128],
+                                           T.t1[:, :, PARTS[p][0] + b:PARTS[p][1]:16], start=b == 0, stop=b == 15),
+                   (("lb16",),) + tuple(("t1", K * i + PARTS[p][0], K * i + PARTS[p][1]) for i in range(3)), (("ph", 24 * p, 24 * p + 24),))
+
+        def first_x(p):
+            o = 24 * p
+            tt(("xq", 8 * p, 8 * p + 8), ("qs", o, o + 8), ("qs", o + 8, o + 16), A.add)
+
+        def first_th(p, i):
+            o, q = 24 * p, (8 * p, 8 * p + 8)
+            if i == 0:
+                ts(("q1",) + q, ("qs", o + 8, o + 16), -32.0, A.mult)
+            else:
+                tt(("thq",) + q, ("q1",) + q, ("qs", o + 16, o + 24), A.subtract)
+
+        def xhot(a0, a1):
+            for a in range(a0, a1):
+                ts(("xh", 64 * a, 64 * a + 64), ("ion",), ("xq", a, a + 1), A.is_equal)
 
         def letter(p):
             p0, p1 = PARTS[p]
@@ -362,12 +410,16 @@ def rank_program(g, core, T, topo):
             for job in late:
                 job()
             late = []
+        def share():
+            op("V", lambda e: e.tensor_copy(v(("cg", 16 * vs, 4096)), v(lex).indirect(v(("hu", vs, K)))), (lex, ("hu", vs, K)), (("cg", 16 * vs, 4096),))
         compare(0)
         mm(("pu1", 0, K), ("id16",), ("h16",))
         for job in late:
             job()
         late = []
         compare(CH)
+        if vs < K:
+            share()
         if PARTS[0][1] == 2 * CH:
             pairs(0)
         compare(2 * CH)
@@ -376,76 +428,98 @@ def rank_program(g, core, T, topo):
         lanes(0)
         compare(3 * CH)
         lanes2(0)
-        places(0)
         pairs(1)
+        lanes3(0)
+        first_q(0)
+        places(0)
         dist(0)
         letter(0)
         lanes(1)
         lanes2(1)
-        to_q(("ph", 0, 48), "lb16", ("t1", 0, 3 * K))
+        cp(("qs", 0, 24), ("ph", 0, 24))
+        lanes3(1)
+        first_x(0)
+        first_th(0, 0)
+        first_q(1)
+        k1 = CFG["xk"]
+        xhot(0, k1)
         places(1)
-        dist(1)
+        first_th(0, 1)
+        if CFG["gv"]:
+            dist_v(1)
+        else:
+            dist(1)
         letter(1)
-        cp(("qs",), ("ph", 0, 48))
-        tt(("xq",), ("qs", 0, 16), ("qs", 16, 32), A.add)
+        cp(("qs", 24, 48), ("ph", 24, 48))
         nx, ns = 16 - CFG["xs"], 16 - CFG["cs"]
+        k2 = min(8, nx)
+        xhot(k1, k1 + 1)
+        first_x(1)
+        first_th(1, 0)
+        xhot(k1 + 1, k1 + 2)
+        first_th(1, 1)
+        xhot(k1 + 2, k2)
         for a in range(nx, 16):
             act(("xa", 64 * a, 64 * a + 64), ("ion",), F.Abs, ("xq", a, a + 1), -1.0)
         act(("xh", 64 * nx, 1024), ("xa", 64 * nx, 1024), F.Relu, 1.0, -1.0)
-        ts(("q1",), ("qs", 16, 32), -32.0, A.mult)
-        ts(("xi",), ("xq",), 64.0, A.mult)
-        tt(("thq",), ("q1",), ("qs", 32, 48), A.subtract)
-        ts(("x3",), ("xi",), 192, A.bitwise_and)
-        for a in range(nx):
-            ts(("xh", 64 * a, 64 * a + 64), ("ion",), ("xq", a, a + 1), A.is_equal)
+        xhot(max(k2, k1 + 2), nx)
         to_q(("pq", 32, 64), "lb", ("ca", 0, 2 * K))
-        cp(("cq",), ("pq", 32, 48))
         tt(("nf",), ("pq", 48, 64), ("thq",), A.is_ge)
+        cp(("cq",), ("pq", 32, 48))
+        ts(("xi",), ("xq",), 64.0, A.mult)
         for a in range(ns, 16):
             act(("xa", 64 * (a - ns), 64 * (a - ns) + 64), ("io0",), F.Abs, ("cq", a, a + 1), -1.0)
         for a in range(ns, 16):
             act(("chh", 64 * a, 64 * a + 64), ("xa", 64 * (a - ns), 64 * (a - ns) + 64), F.Relu, ("nf", a, a + 1), -1.0)
         for a in range(ns):
-            ts(("chh", 64 * a, 64 * a + 64), ("io0",), ("cq", a, a + 1), A.is_equal, ("nf", a, a + 1), A.mult)
+            ts(("chh", 64 * a, 64 * a + 64), ("io0",), ("pq", 32 + a, 33 + a), A.is_equal, ("nf", a, a + 1), A.mult)
         mm(("pxp", K, 2 * K), ("id16",), ("t1", 0, K), True, False)
         mm(("pxp", K, 2 * K), ("nid",), ("ca", 0, K), False, True)
-        mm(("pval", K, 2 * K), ("bo16",), ("t1", 0, K))
+        mm(("pval", K, 2 * K), ("bo16", 0, 128), ("t1", 0, K))
         act(("mt",), ("pval", K, 2 * K), F.Abs, ("nb",))
         act(("rm",), ("mt",), F.Relu, 32768.0, -16384.0)
-        act(("dg2",), ("dg1",), F.Identity, 12582912.0)
+
         for a in range(16):
             x, c = ("xh", 64 * a, 64 * a + 64), ("chh", 64 * a, 64 * a + 64)
             for l, r in ((x, c), (c, x)):
                 op("P", lambda e: e.matmul(T.ph[0:64, 0:64], v(l), v(r), start=a == 0 and l is x, stop=a == 15 and l is c),
                    (l, r), (("ph", 0, 64),))
-        tt(("off",), ("cq",), ("x3",), A.add)
+        ts(("x3",), ("xi",), 192, A.bitwise_and)
         tt(("th2",), ("thq",), ("pq", 48, 64), A.subtract)
-        cp(("of",), ("off",))
+        tt(("x3",), ("pq", 32, 48), ("x3",), A.add)
         tt(("en",), ("pxp", K, 2 * K), ("t1", K, 2 * K), A.mult)
         act(("ndx",), ("en",), F.Relu, None, -1 / 64.0)
-        ts(("q2",), ("th2",), 0.0, A.is_le, 8192.0, A.mult)
-        cp(("hqf",), ("hq",))
-        mm(("ppb", 0, K), ("bo16",), ("eh",))
+        mm(("ppb", 0, K), ("bo16", 0, 128), ("eh",))
         op("V", lambda e: e.tensor_scalar(T.h1[0:64, :], T.ph[0:64, 0:64], 1.0, None, A.min), (("ph", 0, 64),), (("h1",),))
         for q in range(4):
             op("P", lambda e: e.matmul(T.ph[:, K + 64 * q:K + 64 * q + 64], T.ra[0:64, 128 * q:128 * q + 128], T.h1[0:64, :],
                                        start=True, stop=True), (("ra",), ("h1",)), (("ph", K + 64 * q, K + 64 * q + 64),))
         act(("tb",), ("ph", K, 2 * K), F.Copy)
-        tt(("hqx",), ("q2",), ("hqf",), A.add)
-        val = ("pval", 0, K)
-        mm(val, ("bo",), ("ca", K, 2 * K), True, False)
-        mm(val, ("bo16",), ("t1", 2 * K, 3 * K), False, False)
-        mm(val, ("bo16a",), ("t1", K, 2 * K), False, False)
+        cp(("of",), ("x3",))
+        ts(("hr",), ("ppb", 0, K), 2048.0, A.add)
+        ts(("q2",), ("th2",), 0.0, A.is_le, 8192.0, A.mult)
+        cp(("hqf",), ("hq",))
         mm(("pu1", 0, K), ("idn",), XI, True, False)
         mm(("pu1", 0, K), ("idn",), ("ca", 0, K), False, False)
         mm(("pu1", 0, K), ("nid16",), ("t1", 0, K), False, False)
-        mm(("pu1", 0, K), ("nid64",), ("en",), False, True)
+        mm(("pu1", 0, K), ("idx", 0, 128), ("en",), False, True)
+        act(("xb",), ("pu1", 0, K), F.Copy)
+        for p in (0, 1):
+            p0, p1 = PARTS[p]
+            src = ("gs", p0, p1) if p and CFG["gv"] else (("ppa", "ppb")[p], 0, p1 - p0)
+            act(("dg1", p0, p1), src, F.Identity, -0.25, 0.5)
+        act(("dg2",), ("dg1",), F.Identity, 12582912.0)
+        val = ("pval", 0, K)
+        mm(val, ("bo64",), ("ca", K, 2 * K), True, False)
+        mm(val, ("bo16", 128, 256), ("t1", 2 * K, 3 * K), False, False)
+        mm(val, ("bo16", 256, 384), ("t1", K, 2 * K), False, False)
+        mm(val, ("idn",), ("xb",), False, False)
         gat(("f",), ("tb",), ("of",), ("rm",), A.mult)
-        mm(val, ("bo",), ("f",), False, True)
-        ts(("hr",), ("ppb", 0, K), 2048.0, A.add)
-        act(("pu2", K, 2 * K), val, F.Relu, None, -64.0)
-        tt(("yv",), ("ndx",), ("pu2", K, 2 * K), A.min)
-        tt(XO, ("pu1", 0, K), ("yv",), A.subtract)
+        mm(val, ("bo64",), ("f",), False, True)
+        tt(("nx",), ("pu1", 0, K), ("ndx",), A.subtract)
+        tt(("hqx",), ("q2",), ("hqf",), A.add)
+        tt(("yv",), val, ("nx",), A.max)
+        tt(XO, ("yv",), ("pu1", 0, K), A.min)
         send(XO, "xin%d" % (t + 1), "ax%d" % (t + 1))
         act(("pval", K, 2 * K), val, F.Sign, 0.5)
         to_q(("pq", 80, 96), "lb", ("f", 0, K))
@@ -457,35 +531,39 @@ def rank_program(g, core, T, topo):
             act(("ea", e0, e0 + K - 16 * a), ("ppb", 16 * a, K), F.Abs, ("hqs", a, a + 1), -1.0)
         for a in range(nv, 16):
             e0 = 128 * (a - 8)
-            act(("eq", 272 * a, 256 * a + 256), ("ea", e0, e0 + K - 16 * a), F.Relu, 1.0, -1.0)
+            op("S", lambda e: e.activation(T.eq[:, a, 0:K - 16 * a], v(("ea", e0, e0 + K - 16 * a)), F.Relu, bias=1.0, scale=-1.0),
+               (("ea", e0, e0 + K - 16 * a),), (("eq", 272 * a, 256 * a + 256),))
         for a in range(nv):
-            ts(("eq", 272 * a, 256 * a + 256), ("hr", 16 * a, K), ("sq", a, a + 1), A.is_equal)
+            op("V", lambda e: e.tensor_scalar(T.eq[:, a, 0:K - 16 * a], v(("hr", 16 * a, K)), v(("sq", a, a + 1)), None, A.is_equal),
+               (("hr",), ("sq",)), (("eq", 272 * a, 256 * a + 256),))
         tt(("nm",), ("pq", 80, 96), ("th2",), A.is_ge)
         tt(("nm",), ("nm",), ("dmp",), A.mult)
         tt(("hqm",), ("nm",), ("hqf",), A.max)
         mm(("ph", 0, K), ("bo",), ("oz", K, 2 * K), True, False)
         for a in range(15):
-            mm(("ph", 16 * a + 16, K), ("bo",), ("eq", 272 * a + 16, 256 * a + 256), False, False)
-        for b in range(16):
-            op("P", lambda e: e.matmul(T.ph[:, b:K:16], T.blt[:, 128 * b:128 * b + 128], T.eq[:, b:4096:272], start=False, stop=False),
-               (("blt",), ("eq",)), (("ph", 0, K),))
-        mm(("ph", 0, K), ("bo",), ("oz", K, 2 * K), False, True)
+            op("P", lambda e: e.matmul(T.ph[:, 16 * a + 16:K], v(("bo64",)), T.eq[:, a, 16:K - 16 * a], start=False, stop=False),
+               (("bo64",), ("eq", 272 * a, 256 * a + 256)), (("ph", 0, K),))
+        op("P", lambda e: e.matmul(T.ph[:, 0:K], v(("bow",)), T.eq[:, :, 0:16], start=False, stop=True),
+           (("bow",), ("eq", 0, 4096)), (("ph", 0, K),))
         act(("dg",), ("dg2",), F.Identity, -12582912.0)
         tt(("gm",), ("dg",), ("pval", K, 2 * K), A.mult)
-        act(("ls",), ("ph", 0, K), F.Copy, None, 512.0)
+        tt(("ls",), ("ph", 0, K), ("thl",), A.is_ge)
         to_q(("pq", 64, 80), "lb", ("ls", 0, K))
-
-        def new_meanings(GI=GI, GO=GO, t=t):
-            mm(("pu2", 0, K), ("idn",), GI, True, False)
-            mm(("pu2", 0, K), ("idh",), ("dg",), False, False)
-            mm(("pu2", 0, K), ("nidh",), ("gm",), False, True)
-            act(GO, ("pu2", 0, K), F.Copy)
-            send(GO, "gin%d" % (t + 1), "ag%d" % (t + 1))
-        soon.append(new_meanings)
-        tt(("lq2",), ("pq", 64, 80), ("dmp",), A.min)
-        tt(("so0",), ("hqm",), ("lq2",), A.max)
-        cp(("so",), ("so0",))
+        mm(("pxp", K, 2 * K), ("idn",), GI, True, False)
+        mm(("pxp", K, 2 * K), ("idx", 128, 256), ("dg",), False, False)
+        mm(("pxp", K, 2 * K), ("idx", 256, 384), ("gm",), False, True)
+        tt(("lq2",), ("pq", 64, 80), ("dmq",), A.mult)
+        tt(("lq2",), ("hqm",), ("lq2",), A.max)
+        cp(("so",), ("lq2",))
         scat(("lx",), ("so",), XO)
+
+        def new_meanings(GO=GO, t=t):
+            cp(GO, ("pxp", K, 2 * K))
+            send(GO, "gin%d" % (t + 1), "ag%d" % (t + 1))
+        if CFG["go"] and t < NV - 1:
+            soon.append(new_meanings)
+        else:
+            new_meanings()
 
         def meanings(GO=GO):
             scat(("lm",), ("so",), GO)
@@ -494,7 +572,7 @@ def rank_program(g, core, T, topo):
     def store(q, y, a, sem):
         dma(q, lambda e: e.dma_start(y[:], v(a)), sem, (a,), ())
 
-    for job in soon + late:
+    for job in late:
         job()
     arrive("ax%d" % NV, neng, (("xin%d" % NV,),))
     arrive("ag%d" % NV, neng, (("gin%d" % NV,),))

from concourse.mybir import AluOpType as A, ActivationFunctionType as F, AxisListType as X

K = 256
W = 4096
NV = 4
CH = 64
PARTS = ((0, 128), (128, 256))
CFG = {"xs": 6, "cs": 4, "eqs": 6, "chains": (((0, 64),), ((64, 128), (128, 192), (192, 256))), "lm": 1, "gv": 1, "xk": 3, "vs": 16, "go": 1}

SCRATCH = {}


def _buf(name, cols, dtype, where="sbuf", rows=128):
    SCRATCH[name] = (where, [rows, cols], dtype)


for _t in range(NV + 1):
    _buf("xin%d" % _t, K, "bfloat16")
    _buf("gin%d" % _t, K, "bfloat16")
for _d, _l in (
        ("bfloat16", (("xo", NV * K), ("go", NV * K), ("zt", NV * 128), ("lx", W + K), ("lm", W + K), ("ones", 128), ("ones64", 512),
                      ("bo1", 128), ("bo", 128), ("idn", 128), ("lt", 128), ("gt", 128), ("c1", 128), ("c2", 128), ("c3", 128),
                      ("zb", 128), ("za", 128), ("e1", 128), ("bd", 128), ("w1", 256), ("w2", 128), ("lk", 2048), ("lb", 2048),
                      ("bow", 128), ("thl", K), ("nid", 128), ("idx", 384), ("bo64", 128), ("n4096", 256), ("cb", 256), ("xb", K), ("nx", K),
                      ("oz", 512), ("ra", 512), ("io0", 64), ("ion", 64), ("fb", 512), ("cg", 4096), ("d", 4096), ("pair", K),
                      ("ep", K), ("gs", K), ("ca", 2 * K), ("dg", K), ("gm", K), ("en", K), ("ndx", K), ("xa", 1024), ("xh", 1024),
                      ("chh", 1024), ("h1", 64), ("tb", K), ("rm", K), ("f", K), ("ea", 2048), ("ls", K))),
        ("float16", (("lb16", 2048), ("id16", 128), ("nid16", 128), ("bo16", 384), ("h16", K), ("eh", K))),
        ("int32", (("wti", 2), ("thi", 1), ("jci", 1), ("jcj", 1), ("pr", K), ("p2", K), ("h", K), ("xi", 16), ("x3", 16))),
        ("uint16", (("hu", K), ("hq", 16), ("of", 16), ("hr", K), ("so", 16))),
        ("float32", (("thr", NV), ("wf", 2), ("thc", 1), ("jc", 1), ("io16", 16), ("md", 16), ("dm0", 16), ("dmp", 16), ("dmq", 16), ("pw", 16),
                     ("nb", 1), ("u2s", K), ("hqf", 16), ("qs", 48), ("xq", 16), ("q1", 16), ("thq", 16), ("th2", 16), ("q2", 16), ("hqx", 16), ("sq", 16), ("cq", 16),
                     ("nf", 16), ("dg1", K), ("dg2", K), ("mt", K), ("yv", K), ("nm", 16), ("hqm", 16), ("hqs", 16),
                     ("lq2", 16), ("sm", 3)))):
    for _n, _c in _l:
        _buf(_n, _c, _d)
SCRATCH["t1"] = ("sbuf", [128, 3, K], "float16")
SCRATCH["eq"] = ("sbuf", [128, 16, 272], "bfloat16")
for _n in ("pu1", "pu2", "pxp", "ppa", "ppb", "pq", "pval", "ph"):
    _buf(_n, 512, "float32", "psum")

SEMAPHORES = ["v", "s", "p", "gc", "loc"]
SEMAPHORES += ["ld%d" % _i for _i in range(6)] + ["st%d" % _i for _i in range(4)]
SEMAPHORES += ["ax%d" % _i for _i in range(1, NV + 1)] + ["ag%d" % _i for _i in range(1, NV + 1)]


def tracker(g, T):
    queue = {"V": g.vector, "S": g.scalar, "P": g.tensor, "G": g, "Y": g.sync}
    own = {"V": "v", "S": "s", "P": "p", "G": "gc"}
    total = {}
    know = {q: {} for q in queue}
    log = {}

    def span(a):
        if len(a) == 1:
            return a[0], 0, SCRATCH[a[0]][1][1]
        return a

    def need(q, reads, writes):
        found = []
        for wr, accs in ((False, reads), (True, writes)):
            for a in accs:
                name, lo, hi = span(a)
                bank = SCRATCH[name][0] == "psum"
                for r in log.get(name, ()):
                    lap = r["lo"] < hi and lo < r["hi"]
                    if bank and r["q"] != q:
                        found.append(r)
                    elif lap and (r["wr"] or wr):
                        if bank and q == "P":
                            continue
                        found.append(r)
        return found

    def wait(q, found):
        for r in sorted(found, key=lambda r: -r["seq"]):
            if know[q].get(r["sem"], 0) < r["val"]:
                queue[q].wait_ge(T.sem[r["sem"]], r["val"])
                for s, v in r["clock"].items():
                    know[q][s] = max(know[q].get(s, 0), v)

    seq = [0]

    def note(q, sem, val, clock, reads, writes, dma):
        seq[0] += 1
        for wr, accs in ((True, writes), (False, reads)):
            for a in accs:
                name, lo, hi = span(a)
                rows = log.setdefault(name, [])
                if wr:
                    rows[:] = [r for r in rows if not (lo <= r["lo"] and r["hi"] <= hi)]
                rows.append({"q": q, "sem": sem, "val": val, "clock": clock, "lo": lo, "hi": hi, "wr": wr, "dma": dma, "seq": seq[0]})

    def op(q, call, reads=(), writes=()):
        wait(q, need(q, reads, writes))
        sem = own[q]
        call(queue[q]).then_inc(T.sem[sem], 1)
        total[sem] = total.get(sem, 0) + 1
        clock = dict(know[q])
        clock[sem] = total[sem]
        note(q, sem, total[sem], clock, reads, writes, False)

    def dma(q, call, sem, reads=(), writes=()):
        wait(q, need(q, reads, writes))
        call(queue[q]).then_inc(T.sem[sem], 16)
        clock = dict(know[q])
        clock[sem] = 16
        note("dma", sem, 16, clock, reads, writes, True)

    def arrive(sem, val, writes):
        note("dma", sem, val, {sem: val}, (), writes, True)

    def ready(q, reads):
        wait(q, need(q, reads, ()))

    def finish():
        for sem, q in (("v", "G"), ("s", "G"), ("p", "G"), ("gc", "V")):
            if know[q].get(sem, 0) < total[sem]:
                queue[q].wait_ge(T.sem[sem], total[sem])

    return op, dma, arrive, ready, finish


def rank_program(g, core, T, topo):
    rank = T.rank_of(core)
    if rank is None:
        return
    op, dma, arrive, ready, finish = tracker(g, T)

    def v(a):
        if a[0] == "t1":
            return T.t1[:, a[1] // K, a[1] % K:a[1] % K + a[2] - a[1]]
        return T[a[0]][:] if len(a) == 1 else T[a[0]][:, a[1]:a[2]] if len(a) == 3 else T[a[0]][:, a[1]:a[2]:a[3]]

    def rw(*a):
        return tuple(x[:3] for x in a if isinstance(x, tuple))

    def sc(x):
        return v(x) if isinstance(x, tuple) else x

    def ts(out, i0, s1, o0, s2=None, o1=None):
        if o1 is None:
            op("V", lambda e: e.tensor_scalar(v(out), v(i0), sc(s1), None, o0), rw(i0, s1), rw(out))
        else:
            op("V", lambda e: e.tensor_scalar(v(out), v(i0), sc(s1), sc(s2), o0, o1), rw(i0, s1, s2), rw(out))

    def tt(out, a, b, o):
        op("V", lambda e: e.tensor_tensor(v(out), v(a), v(b), o), rw(a, b), rw(out))

    def gat(out, win, offs, b, o):
        op("V", lambda e: e.tensor_tensor(v(out), v(win).indirect(v(offs)), v(b), o), rw(win, offs, b), rw(out))

    def cp(out, a):
        op("V", lambda e: e.tensor_copy(v(out), v(a)), rw(a), rw(out))

    def scat(win, offs, a):
        op("V", lambda e: e.tensor_copy(v(win).indirect(v(offs)), v(a)), rw(offs, a), rw(win))

    def fill(out, c):
        op("V", lambda e: e.memset(v(out), c), (), rw(out))

    def act(out, a, fn, bias=None, scale=None, offs=None, acc=None):
        kw = {}
        if bias is not None:
            kw["bias"] = sc(bias)
        if scale is not None:
            kw["scale"] = scale
        if acc is not None:
            kw["accum_out"] = v(acc)
        src = v(a) if offs is None else v(a).indirect(v(offs))
        op("S", lambda e: e.activation(v(out), src, fn, **kw), rw(a, bias, offs), rw(out, acc))

    def mm(out, l, rh, st=True, sp=True):
        op("P", lambda e: e.matmul(v(out), v(l), v(rh), start=st, stop=sp), rw(l, rh), rw(out))

    def to_q(out, lname, src, st=True, sp=True):
        for b in range(16):
            op("P", lambda e: e.matmul(v(out), T[lname][:, 128 * b:128 * b + 128], T[src[0]][:, src[1] + b:src[2]:16],
                                       start=st and b == 0, stop=sp and b == 15), ((lname,), src), rw(out))

    def load(q, out, src, sem):
        dma(q, lambda e: e.dma_start(v(out), src[:]), sem, (), (out,))

    load("S", ("xin0",), T.xw, "ld0")
    load("Y", ("wti",), T.wts, "ld1")
    load("Y", ("lx", 0, W), T.lex, "ld2")
    load("S", ("thi",), T.th, "ld3")
    load("Y", ("gin0",), T.gw, "ld4")
    load("Y", ("lm", 0, W), T.mng, "ld5")

    fill(("ones",), 1.0)
    fill(("ones64",), 1.0)

    def sel(out, i, pat, o, base, cm, rows=128):
        op("G", lambda e: e.affine_select(T[out][0:rows, :], T[i][0:rows, :], pat, o, 0.0, base, cm), ((i,),), ((out,),))

    def iota(out, pat, base, cm, **kw):
        op("G", lambda e: e.iota(T[out][:], pat, base, cm, **kw), (), ((out,),))

    small = {"allow_small_or_imprecise_dtypes": True}
    sel("bo1", "ones", [[-16, 8], [0, 16]], A.is_ge, 0, 1)
    sel("bo", "bo1", [[16, 8], [0, 16]], A.is_ge, 15, -1)
    sel("idn", "ones", [[-1, 128]], A.is_equal, 0, 1)
    iota("jci", [[0, 1]], 0, 1)
    iota("io16", [[1, 16]], 0, 0, **small)
    sel("lt", "bo", [[1, 128]], A.is_gt, 0, -1)
    sel("gt", "bo", [[-1, 128]], A.is_gt, 0, 1)
    iota("io0", [[1, 64]], 0, 0, **small)
    iota("ion", [[1, 64]], -64, 0, **small)
    iota("dm0", [[16, 16]], W, 0, **small)
    sel("ra", "ones64", [[-1, 4], [0, 8], [-4, 16]], A.is_equal, 0, 1, 64)

    fill(("cb", 0, 128), 4160.0)
    fill(("cb", 128, 256), 67584.0)
    fill(("oz", 0, K), 1.0)
    fill(("oz", K, 2 * K), 0.0)
    fill(("lk",), 0.0)
    ts(("n4096", 0, 128), ("idn",), -4096.0, A.mult)
    ts(("n4096", 128, 256), ("idn",), -131072.0, A.mult)
    tt(("bd",), ("bo",), ("idn",), A.subtract)
    ts(("c1",), ("idn",), -17.0, A.mult)
    cp(("wf",), ("wti",))
    ts(("w1", 0, 128), ("bd",), ("wf", 0, 1), A.mult)
    ts(("w2",), ("bd",), ("wf", 1, 2), A.mult)
    ts(("w1", 128, 256), ("bd",), ("wf", 0, 1), A.mult, 32.0, A.mult)
    tt(("e1",), ("bo",), ("c1",), A.add)
    fill(("lb",), 0.0)

    def blocks(out, src):
        for k in range(16):
            act((out, 128 * k + k, 128 * (k + 1), 16), (src, k, 128, 16), F.Copy)

    def consts2():
        ts(("c2",), ("lt",), 2.0, A.mult)
        ts(("c3",), ("lt",), 64.0, A.mult)
        tt(("zb",), ("c2",), ("idn",), A.subtract)
        tt(("c2",), ("c3",), ("c1",), A.add)
        tt(("za",), ("c2",), ("gt",), A.add)
        for t in range(NV):
            act(("zt", 128 * t, 128 * t + 128), ("zb",), F.Copy)
        for t in range(NV):
            act(("zt", 128 * t + t, 128 * t + 128, 16), ("za", t, 128, 16), F.Copy)
        ts(("jcj",), ("jci",), 15, A.bitwise_and)
        cp(("id16",), ("idn",))
        cp(("jc",), ("jcj",))
        ts(("thc",), ("thi",), -2048.0, A.add, 1 / 64.0, A.mult)
        ts(("md",), ("io16",), ("jc",), A.is_equal)
        ts(("thr",), ("md", 0, NV), -0.5, A.add)

    def consts3():
        cp(("lb16",), ("lb",))
        ts(("nid",), ("idn",), -1.0, A.mult)
        cp(("bo16", 0, 128), ("bo",))
        ts(("bo16", 128, 256), ("bo",), 64.0, A.mult)
        ts(("bo16", 256, 384), ("bo",), 2048.0, A.mult)
        ts(("bo64",), ("bo",), 64.0, A.mult)
        ts(("nb",), ("jc",), -4.0, A.mult, -1.5, A.add)
        ts(("nid16",), ("idn",), -1.0, A.mult)
        for i, c in enumerate((-1 / 64.0, 0.5, -0.5)):
            ts(("idx", 128 * i, 128 * i + 128), ("idn",), c, A.mult)
        ts(("dmp",), ("dm0",), ("jc",), A.add)
        ts(("dmq",), ("dmp",), 1 / 16.0, A.mult)

    def consts4():
        fill(("rm",), 0.5)
        fill(("rm", 0, K, 16), 32768.0)
        op("V", lambda e: e.tensor_tensor_scan(v(("thl",)), v(("rm",)), v(("oz", K, 2 * K)), 2.0 ** -13, A.mult, A.add),
           (("rm",), ("oz", K, 2 * K)), (("thl",),))
        tt(("pw",), ("md",), ("thl", 0, 16), A.mult)
        op("V", lambda e: e.tensor_reduce(v(("sm", 0, 1)), v(("pw",)), X.X, A.add), (("pw",),), (("sm", 0, 1),))
        ts(("bow",), ("bo",), ("sm", 0, 1), A.mult, 0.5, A.mult)

    nxt = T.cores[(rank + 1) % len(T.cores)]
    rid, pid = topo.addr(nxt)[0], topo.addr(nxt)[1]
    mask = topo.mask(core, nxt)
    neng = len(topo.engines(core, nxt))

    def send(src, dst, sem):
        ready("G", (src,))
        g.remote_dma(T[dst][:], v(src), T.sem[sem], T.sem.loc, pid, rid, mask)

    lex, mng = ("lx", 0, W), ("lm", 0, W)
    soon = []
    late = [consts3, consts4]

    for t in range(NV):
        XI, GI = ("xin%d" % t,), ("gin%d" % t,)
        XO, GO = ("xo", K * t, K * t + K), ("go", K * t, K * t + K)
        if t:
            arrive("ax%d" % t, neng, (XI,))
            arrive("ag%d" % t, neng, (GI,))
        wide = ((0, CH, "pu1", "ppa", "pval"), (CH, K, "pu2", "ph", "ppb"))
        for c0, c1, bu, b2, b1 in wide:
            n = c1 - c0
            for i, w in ((1, ("w2",)), (0, ("w1", 0, 128))):
                mm((bu, n * (1 - i), n * (2 - i)), w, ("xin%d" % t, c0, c1))
            for i in (1, 0):
                act(("fb", K * i + c0, K * i + c1), (bu, n * (1 - i), n * (2 - i)), F.Identity, 130 - 2047.5 / 4096, 1 / 4096.0)
        for c0, c1, bu, b2, b1 in wide:
            n = c1 - c0
            for r, i, q, w in (((b2, 0, n), 1, 0, ("w2",)), ((b1, 0, n), 0, 0, ("w1", 0, 128)), ((b1, n, 2 * n), 0, 128, ("w1", 128, 256))):
                mm(r, ("cb", q, q + 128), ("oz", 0, n), True, False)
                mm(r, w, ("xin%d" % t, c0, c1), False, False)
                mm(r, ("n4096", q, q + 128), ("fb", K * i + c0, K * i + c1), False, True)
            act(("u2s", c0, c1), (b2, 0, n), F.Copy)
        mm(("pxp", 0, K), ("idn",), XI)

        def um(c0, c1, q):
            b, o, n = ("pval", 0, CH) if c1 <= CH else ("ppb", CH, K - CH)
            return (b, c0 - o + n * q, c1 - o + n * q)

        for chain in CFG["chains"]:
            for c0, c1 in chain:
                tt(("pr", c0, c1), ("u2s", c0, c1), um(c0, c1, 0), A.mult)
            for c0, c1 in chain:
                tt(("p2", c0, c1), ("pr", c0, c1), um(c0, c1, 1), A.add)
            for c0, c1 in chain:
                ts(("h", c0, c1), ("p2", c0, c1), 5, A.arith_shift_right, 4095, A.bitwise_and)
            for c0, c1 in chain:
                cp(("hu", c0, c1), ("h", c0, c1))
            for job in soon:
                job()
            soon = []
        if t == 0:
            blocks("lk", "e1")
            blocks("lb", "bo")
            consts2()
        vs = K - CFG["vs"]
        for c in range(0, K, CH):
            e1 = min(c + CH, vs)
            act(("cg", 16 * c, 16 * e1), lex, F.Copy, offs=("hu", c, e1))

        def compare(c):
            bank = "ppa" if c < PARTS[0][1] else "ppb"
            o = c - (0 if bank == "ppa" else PARTS[1][0])
            for k in range(16):
                d0 = 16 * c + k * CH
                tt(("d", d0, d0 + CH), ("cg", 16 * c + k, 16 * (c + CH), 16), ("pxp", c, c + CH), A.not_equal)
            for k in range(16):
                d0 = 16 * c + k * CH
                mm((bank, o, o + CH), ("lk", 128 * k, 128 * k + 128), ("d", d0, d0 + CH), k == 0, k == 15)

        def pairs(p):
            p0, p1 = PARTS[p]
            bank, n = ("ppa", "ppb")[p], p1 - p0
            ts(("pair", p0, p1), (bank, 0, n), -13.5, A.is_lt)
            mm((bank, n, 2 * n), ("zt", 128 * t, 128 * t + 128), ("pair", p0, p1))

        def lanes(p):
            p0, p1 = PARTS[p]
            bank, n = ("ppa", "ppb")[p], p1 - p0
            ts(("ep", p0, p1), (bank, n, 2 * n), ("thr", t, t + 1), A.is_lt)
            tt(("eh", p0, p1), ("ep", p0, p1), ("pu1", p0, p1), A.mult)
            to_q(("pq", p0 // 16, p1 // 16), "lb16", ("eh", p0, p1))

        def lanes2(p):
            p0, p1 = PARTS[p]
            bank, n = ("ppa", "ppb")[p], p1 - p0
            ts(("t1", K + p0, K + p1), (bank, n, 2 * n), -0.5, A.is_lt, -64.0, A.mult)
            tt(("t1", p0, p1), ("ep", p0, p1), ("pxp", p0, p1), A.mult)

        def lanes3(p):
            p0, p1 = PARTS[p]
            ts(("t1", 2 * K + p0, 2 * K + p1), ("t1", K + p0, K + p1), ("thc",), A.mult)

        def places(p):
            a0, a1 = PARTS[p][0] // 16, PARTS[p][1] // 16
            ts(("hq", a0, a1), ("pq", a0, a1), 2048.0, A.add)

        def dist(p):
            p0, p1 = PARTS[p]
            bank, n = ("ppa", "ppb")[p], p1 - p0
            act(("gs", p0, p1), mng, F.Copy, offs=("hq", p0 // 16, p1 // 16))
            mm((bank, 0, n), ("nid",), ("gin%d" % t, p0, p1), True, False)
            mm((bank, 0, n), ("idn",), ("gs", p0, p1), False, True)
            act(("ca", K + p0, K + p1), (bank, 0, n), F.Abs)

        def dist_v(p):
            p0, p1 = PARTS[p]
            gat(("gs", p0, p1), mng, ("hq", p0 // 16, p1 // 16), ("gin%d" % t, p0, p1), A.subtract)
            act(("ca", K + p0, K + p1), ("gs", p0, p1), F.Abs)

        def first_q(p):
            for b in range(16):
                op("P", lambda e: e.matmul(T.ph[:, 24 * p:24 * p + 24], T.lb16[:, 128 * b:128 * b + 128],
                                           T.t1[:, :, PARTS[p][0] + b:PARTS[p][1]:16], start=b == 0, stop=b == 15),
                   (("lb16",),) + tuple(("t1", K * i + PARTS[p][0], K * i + PARTS[p][1]) for i in range(3)), (("ph", 24 * p, 24 * p + 24),))

        def first_x(p):
            o = 24 * p
            tt(("xq", 8 * p, 8 * p + 8), ("qs", o, o + 8), ("qs", o + 8, o + 16), A.add)

        def first_th(p, i):
            o, q = 24 * p, (8 * p, 8 * p + 8)
            if i == 0:
                ts(("q1",) + q, ("qs", o + 8, o + 16), -32.0, A.mult)
            else:
                tt(("thq",) + q, ("q1",) + q, ("qs", o + 16, o + 24), A.subtract)

        def xhot(a0, a1):
            for a in range(a0, a1):
                ts(("xh", 64 * a, 64 * a + 64), ("ion",), ("xq", a, a + 1), A.is_equal)

        def letter(p):
            p0, p1 = PARTS[p]
            gat(("ca", p0, p1), lex, ("hq", p0 // 16, p1 // 16), ("ep", p0, p1), A.mult)

        ts(("h16",), ("hu",), -2048.0, A.add)
        if CFG["lm"] or not t:
            for job in late:
                job()
            late = []
        def share():
            op("V", lambda e: e.tensor_copy(v(("cg", 16 * vs, 4096)), v(lex).indirect(v(("hu", vs, K)))), (lex, ("hu", vs, K)), (("cg", 16 * vs, 4096),))
        compare(0)
        mm(("pu1", 0, K), ("id16",), ("h16",))
        for job in late:
            job()
        late = []
        compare(CH)
        if vs < K:
            share()
        if PARTS[0][1] == 2 * CH:
            pairs(0)
        compare(2 * CH)
        if PARTS[0][1] == 3 * CH:
            pairs(0)
        lanes(0)
        compare(3 * CH)
        lanes2(0)
        pairs(1)
        lanes3(0)
        first_q(0)
        places(0)
        dist(0)
        letter(0)
        lanes(1)
        lanes2(1)
        cp(("qs", 0, 24), ("ph", 0, 24))
        lanes3(1)
        first_x(0)
        first_th(0, 0)
        first_q(1)
        k1 = CFG["xk"]
        xhot(0, k1)
        places(1)
        first_th(0, 1)
        if CFG["gv"]:
            dist_v(1)
        else:
            dist(1)
        letter(1)
        cp(("qs", 24, 48), ("ph", 24, 48))
        nx, ns = 16 - CFG["xs"], 16 - CFG["cs"]
        k2 = min(8, nx)
        xhot(k1, k1 + 1)
        first_x(1)
        first_th(1, 0)
        xhot(k1 + 1, k1 + 2)
        first_th(1, 1)
        xhot(k1 + 2, k2)
        for a in range(nx, 16):
            act(("xa", 64 * a, 64 * a + 64), ("ion",), F.Abs, ("xq", a, a + 1), -1.0)
        act(("xh", 64 * nx, 1024), ("xa", 64 * nx, 1024), F.Relu, 1.0, -1.0)
        xhot(max(k2, k1 + 2), nx)
        to_q(("pq", 32, 64), "lb", ("ca", 0, 2 * K))
        tt(("nf",), ("pq", 48, 64), ("thq",), A.is_ge)
        cp(("cq",), ("pq", 32, 48))
        ts(("xi",), ("xq",), 64.0, A.mult)
        for a in range(ns, 16):
            act(("xa", 64 * (a - ns), 64 * (a - ns) + 64), ("io0",), F.Abs, ("cq", a, a + 1), -1.0)
        for a in range(ns, 16):
            act(("chh", 64 * a, 64 * a + 64), ("xa", 64 * (a - ns), 64 * (a - ns) + 64), F.Relu, ("nf", a, a + 1), -1.0)
        for a in range(ns):
            ts(("chh", 64 * a, 64 * a + 64), ("io0",), ("pq", 32 + a, 33 + a), A.is_equal, ("nf", a, a + 1), A.mult)
        mm(("pxp", K, 2 * K), ("id16",), ("t1", 0, K), True, False)
        mm(("pxp", K, 2 * K), ("nid",), ("ca", 0, K), False, True)
        mm(("pval", K, 2 * K), ("bo16", 0, 128), ("t1", 0, K))
        act(("mt",), ("pval", K, 2 * K), F.Abs, ("nb",))
        act(("rm",), ("mt",), F.Relu, 32768.0, -16384.0)

        for a in range(16):
            x, c = ("xh", 64 * a, 64 * a + 64), ("chh", 64 * a, 64 * a + 64)
            for l, r in ((x, c), (c, x)):
                op("P", lambda e: e.matmul(T.ph[0:64, 0:64], v(l), v(r), start=a == 0 and l is x, stop=a == 15 and l is c),
                   (l, r), (("ph", 0, 64),))
        ts(("x3",), ("xi",), 192, A.bitwise_and)
        tt(("th2",), ("thq",), ("pq", 48, 64), A.subtract)
        tt(("x3",), ("pq", 32, 48), ("x3",), A.add)
        tt(("en",), ("pxp", K, 2 * K), ("t1", K, 2 * K), A.mult)
        act(("ndx",), ("en",), F.Relu, None, -1 / 64.0)
        mm(("ppb", 0, K), ("bo16", 0, 128), ("eh",))
        op("V", lambda e: e.tensor_scalar(T.h1[0:64, :], T.ph[0:64, 0:64], 1.0, None, A.min), (("ph", 0, 64),), (("h1",),))
        for q in range(4):
            op("P", lambda e: e.matmul(T.ph[:, K + 64 * q:K + 64 * q + 64], T.ra[0:64, 128 * q:128 * q + 128], T.h1[0:64, :],
                                       start=True, stop=True), (("ra",), ("h1",)), (("ph", K + 64 * q, K + 64 * q + 64),))
        act(("tb",), ("ph", K, 2 * K), F.Copy)
        cp(("of",), ("x3",))
        ts(("hr",), ("ppb", 0, K), 2048.0, A.add)
        ts(("q2",), ("th2",), 0.0, A.is_le, 8192.0, A.mult)
        cp(("hqf",), ("hq",))
        mm(("pu1", 0, K), ("idn",), XI, True, False)
        mm(("pu1", 0, K), ("idn",), ("ca", 0, K), False, False)
        mm(("pu1", 0, K), ("nid16",), ("t1", 0, K), False, False)
        mm(("pu1", 0, K), ("idx", 0, 128), ("en",), False, True)
        act(("xb",), ("pu1", 0, K), F.Copy)
        for p in (0, 1):
            p0, p1 = PARTS[p]
            src = ("gs", p0, p1) if p and CFG["gv"] else (("ppa", "ppb")[p], 0, p1 - p0)
            act(("dg1", p0, p1), src, F.Identity, -0.25, 0.5)
        act(("dg2",), ("dg1",), F.Identity, 12582912.0)
        val = ("pval", 0, K)
        mm(val, ("bo64",), ("ca", K, 2 * K), True, False)
        mm(val, ("bo16", 128, 256), ("t1", 2 * K, 3 * K), False, False)
        mm(val, ("bo16", 256, 384), ("t1", K, 2 * K), False, False)
        mm(val, ("idn",), ("xb",), False, False)
        gat(("f",), ("tb",), ("of",), ("rm",), A.mult)
        mm(val, ("bo64",), ("f",), False, True)
        tt(("nx",), ("pu1", 0, K), ("ndx",), A.subtract)
        tt(("hqx",), ("q2",), ("hqf",), A.add)
        tt(("yv",), val, ("nx",), A.max)
        tt(XO, ("yv",), ("pu1", 0, K), A.min)
        send(XO, "xin%d" % (t + 1), "ax%d" % (t + 1))
        act(("pval", K, 2 * K), val, F.Sign, 0.5)
        to_q(("pq", 80, 96), "lb", ("f", 0, K))
        nv = 16 - CFG["eqs"]
        tt(("sq",), ("hqx",), ("pq", 80, 96), A.add)
        ts(("hqs", nv, 16), ("sq", nv, 16), -2048.0, A.add)
        for a in range(nv, 16):
            e0 = 128 * (a - 8)
            act(("ea", e0, e0 + K - 16 * a), ("ppb", 16 * a, K), F.Abs, ("hqs", a, a + 1), -1.0)
        for a in range(nv, 16):
            e0 = 128 * (a - 8)
            op("S", lambda e: e.activation(T.eq[:, a, 0:K - 16 * a], v(("ea", e0, e0 + K - 16 * a)), F.Relu, bias=1.0, scale=-1.0),
               (("ea", e0, e0 + K - 16 * a),), (("eq", 272 * a, 256 * a + 256),))
        for a in range(nv):
            op("V", lambda e: e.tensor_scalar(T.eq[:, a, 0:K - 16 * a], v(("hr", 16 * a, K)), v(("sq", a, a + 1)), None, A.is_equal),
               (("hr",), ("sq",)), (("eq", 272 * a, 256 * a + 256),))
        tt(("nm",), ("pq", 80, 96), ("th2",), A.is_ge)
        tt(("nm",), ("nm",), ("dmp",), A.mult)
        tt(("hqm",), ("nm",), ("hqf",), A.max)
        mm(("ph", 0, K), ("bo",), ("oz", K, 2 * K), True, False)
        for a in range(15):
            op("P", lambda e: e.matmul(T.ph[:, 16 * a + 16:K], v(("bo64",)), T.eq[:, a, 16:K - 16 * a], start=False, stop=False),
               (("bo64",), ("eq", 272 * a, 256 * a + 256)), (("ph", 0, K),))
        op("P", lambda e: e.matmul(T.ph[:, 0:K], v(("bow",)), T.eq[:, :, 0:16], start=False, stop=True),
           (("bow",), ("eq", 0, 4096)), (("ph", 0, K),))
        act(("dg",), ("dg2",), F.Identity, -12582912.0)
        tt(("gm",), ("dg",), ("pval", K, 2 * K), A.mult)
        tt(("ls",), ("ph", 0, K), ("thl",), A.is_ge)
        to_q(("pq", 64, 80), "lb", ("ls", 0, K))
        mm(("pxp", K, 2 * K), ("idn",), GI, True, False)
        mm(("pxp", K, 2 * K), ("idx", 128, 256), ("dg",), False, False)
        mm(("pxp", K, 2 * K), ("idx", 256, 384), ("gm",), False, True)
        tt(("lq2",), ("pq", 64, 80), ("dmq",), A.mult)
        tt(("lq2",), ("hqm",), ("lq2",), A.max)
        cp(("so",), ("lq2",))
        scat(("lx",), ("so",), XO)

        def new_meanings(GO=GO, t=t):
            cp(GO, ("pxp", K, 2 * K))
            send(GO, "gin%d" % (t + 1), "ag%d" % (t + 1))
        if CFG["go"] and t < NV - 1:
            soon.append(new_meanings)
        else:
            new_meanings()

        def meanings(GO=GO):
            scat(("lm",), ("so",), GO)
        late.append(meanings)

    def store(q, y, a, sem):
        dma(q, lambda e: e.dma_start(y[:], v(a)), sem, (a,), ())

    for job in late:
        job()
    arrive("ax%d" % NV, neng, (("xin%d" % NV,),))
    arrive("ag%d" % NV, neng, (("gin%d" % NV,),))
    store("Y", T.yx, ("xin%d" % NV,), "st1")
    store("Y", T.yl, lex, "st0")
    store("Y", T.yg, ("gin%d" % NV,), "st2")
    h = W // 2
    op("V", lambda e: e.tensor_reduce(T.sm[:, 0:1], T.lm[:, 0:h], X.X, A.add), (("lm", 0, h),), (("sm", 0, 1),))
    act(("cg", 0, h), ("lm", h, W), F.Copy, acc=("sm", 1, 2))
    tt(("sm", 2, 3), ("sm", 0, 1), ("sm", 1, 2), A.add)
    store("S", T.ym, ("sm", 2, 3), "st3")
    for i in range(4):
        g.wait_ge(T.sem["st%d" % i], 16)
    g.wait_ge(T.sem.loc, 2 * NV * neng)
    finish()
